import numpy as np
import ml_dtypes


def mxq(x, axis, fmt="e4m3"):
    dtype, down = {"e4m3": (ml_dtypes.float8_e4m3fn, 7), "e5m2": (ml_dtypes.float8_e5m2, 14)}[fmt]
    v = np.moveaxis(np.asarray(x, np.float32).astype(ml_dtypes.bfloat16).astype(np.float64), axis, -1)
    blocks = v.reshape(v.shape[:-1] + (-1, 32))
    amax = np.abs(blocks).max(-1, keepdims=True)
    byte = np.maximum(np.where(amax > 0, np.frexp(amax)[1] - 1 + 127, 0) - down, 1)
    scale = np.exp2(byte - 127.0)
    codes = (blocks / scale).astype(np.float32).astype(dtype).astype(np.float64)
    return np.moveaxis((codes * scale).reshape(v.shape), -1, axis)


WIDE = False


def mx_kscale(k):
    if not WIDE:
        return np.ones(k)
    levels = np.array([24, -24, 12, -12, 0])
    if k % 512:
        return np.exp2(np.random.permutation(np.resize(levels, k // 32))).repeat(32)
    a = np.empty((k // 512, 16))
    for p in range(k // 512):
        a[p, :8] = np.random.permutation(np.resize(levels, 8))
        for g in range(8):
            far = levels[np.abs(levels - a[p, g]) >= 10]
            a[p, g + 8] = far[np.random.randint(len(far))]
    return np.exp2(a.ravel()).repeat(32)


def f64(x):
    return np.asarray(x).astype(np.float64)


def striped(idx):
    return np.tile(idx.reshape(-1, 16).T, (8, 1)).astype(np.uint16)


def unstriped(offs):
    return offs[:16].T.reshape(-1).astype(np.int64)


E2M1 = np.array([0.0, 0.5, 1.0, 1.5, 2.0, 3.0, 4.0, 6.0, -0.0, -0.5, -1.0, -1.5, -2.0, -3.0, -4.0, -6.0])


def pack_weight(w, fmt):
    k, n = w.shape
    w = f64(np.asarray(w, np.float32).astype(ml_dtypes.bfloat16)).reshape(k // 32, 32, n)
    amax = np.abs(w).max(1)
    if fmt == "e4m3":
        byte = np.frexp(amax)[1] - 1 + 127 - 7
    else:
        mant, ex = np.frexp(amax / 6.0)
        byte = np.where(mant > 0.5, ex, ex - 1) + 127
    byte = np.clip(np.where(amax > 0, byte, 1), 1, 254)
    scaled = (w * np.exp2(127.0 - byte)[:, None, :]).reshape(k, n).astype(np.float32)
    by_word = np.ascontiguousarray(scaled.reshape(k // 512, 128, 4, n).transpose(0, 1, 3, 2))
    if fmt == "e4m3":
        words = by_word.astype(ml_dtypes.float8_e4m3fn).view(np.uint8)
    else:
        c = by_word.astype(ml_dtypes.float4_e2m1fn).view(np.uint8) & 0xF
        words = (c[..., 0::2] | (c[..., 1::2] << 4)).reshape(k // 512, 128, 2 * n)
    return np.ascontiguousarray(words), np.ascontiguousarray(byte.astype(np.uint8).reshape(k // 512, 16, n))


def unpack_weight(words, scales, fmt):
    g, _, n = scales.shape
    words = np.ascontiguousarray(words).reshape(g, 128, n, -1)
    if fmt == "e4m3":
        vals = words.view(ml_dtypes.float8_e4m3fn).astype(np.float64)
    else:
        nib = np.empty((g, 128, n, 4), np.uint8)
        nib[..., 0::2] = words & 0xF
        nib[..., 1::2] = words >> 4
        vals = E2M1[nib]
    vals = vals * np.repeat(np.exp2(scales.astype(np.float64) - 127.0), 8, axis=1)[..., None]
    return vals.transpose(0, 1, 3, 2).reshape(g * 512, n)


def pack_table4(v):
    words, scales = pack_weight(v, "e2m1")
    g, t = words.shape[0] // 2, v.shape[1]
    return np.ascontiguousarray(words.reshape(g, 2, 128, t, 2).transpose(0, 2, 3, 1, 4).reshape(g, 128, t, 4)), scales


def unpack_table4(words, scales):
    g, _, t, _ = words.shape
    return unpack_weight(words.reshape(g, 128, t, 2, 2).transpose(0, 3, 1, 2, 4).reshape(2 * g, 128, 2 * t), scales, "e2m1")


def planes(y):
    n, m = y.shape
    v = y.astype(np.float32).astype(ml_dtypes.bfloat16).astype(np.float64).reshape(n // 32, 32, m)
    top = np.abs(v).max(1)
    byte = np.clip(np.where(top > 0, np.frexp(top)[1] - 1 + 127 - 7, 1), 1, 254)
    codes = (v * np.exp2(127.0 - byte)[:, None, :]).reshape(n, m).astype(np.float32).astype(ml_dtypes.float8_e4m3fn).view(np.uint8)
    words = codes.reshape(n // 512, 128, 4, m).transpose(0, 1, 3, 2)
    return np.ascontiguousarray(words), np.ascontiguousarray(byte.astype(np.uint8).reshape(n // 512, 16, m))


def silu(f):
    return f / (1.0 + np.exp(-np.maximum(f, -700.0)))


K, R, N, T, J = 1024, 1024, 512, 2048, 1024


def setup_inputs():
    n = np.random.standard_normal
    s = mx_kscale(K)[:, None]
    u = mx_kscale(R)[:, None]
    p_tab = pack_table4(n((K, T)) * s)
    p_wu = pack_weight(n((K, R)) / np.sqrt(K) / s * u.T, "e4m3")
    p_wd = pack_weight(n((R, N)) / np.sqrt(R) / u, "e2m1")
    return {
        "tab_words": p_tab[0],
        "tab_scales": p_tab[1],
        "wg": (n((K, R)) / np.sqrt(K) / s).astype(np.float32),
        "wu_words": p_wu[0],
        "wu_scales": p_wu[1],
        "wd_words": p_wd[0],
        "wd_scales": p_wd[1],
        "gT": (n((N, T))).astype(np.float32),
        "wgo": np.tile(np.random.uniform(0.5, 2.0, J), (128, 1)).astype(np.float32),
        "offs": striped(np.random.permutation(T)[:J]),
    }


def reference(tab_words, tab_scales, wg, wu_words, wu_scales, wd_words, wd_scales, gT, wgo, offs):
    idx = unstriped(offs)
    tab_ = unpack_table4(tab_words, tab_scales)[:, idx]
    wg_ = mxq(f64(wg), 0, "e4m3")
    wu_ = unpack_weight(wu_words, wu_scales, "e4m3")
    ga = wg_.T @ tab_
    ub = wu_.T @ tab_
    h = silu(ga) * ub
    h_ = mxq(h, 0, "e4m3")
    wd_ = unpack_weight(wd_words, wd_scales, "e2m1")
    y = wd_.T @ h_
    out = np.zeros((N, T))
    out[:, idx] = f64(wgo)[0] * (y * f64(gT)[:, idx])
    return (out,) + planes(out)

@@ -1,0 +1,283 @@
+from contextlib import ExitStack
+
+import concourse.mybir as mybir
+
+K, R, N, T, J = 1024, 1024, 512, 2048, 1024
+FLOPS = 2 * J * (2 * K * R + R * N)
+
+F32 = mybir.dt.float32
+BF16 = mybir.dt.bfloat16
+I32 = mybir.dt.int32
+U32 = mybir.dt.uint32
+U16 = mybir.dt.uint16
+U8 = mybir.dt.uint8
+FP8X4 = mybir.dt.float8_e4m3fn_x4
+FP4X4 = mybir.dt.float4_e2m1fn_x4
+MULT = mybir.AluOpType.mult
+SILU = mybir.ActivationFunctionType.Silu
+
+P = 128
+PACK = 4
+PASS = P * PACK
+QUAD = 32
+HALF = J // 2
+PIECE = 512
+
+
+def tile_list_modp_gsilu_gateP_kernel(
+    tc, tab_words, tab_scales, wg, wu_words, wu_scales, wd_words, wd_scales, gT, wgo, offs, out_0, out_1, out_2
+):
+    nc = tc.nc
+    with ExitStack() as ctx:
+        keep = ctx.enter_context(tc.tile_pool(name="keep", bufs=1))
+        ring = ctx.enter_context(tc.tile_pool(name="ring", bufs=3))
+        psum = ctx.enter_context(tc.psum_pool(name="psum", bufs=1))
+
+        def sb(name, shape, dtype, tag=None):
+            return keep.tile(shape, dtype, name=name, tag=tag or name, align_bytes=64)
+
+        offsets = keep.tile([P, J // 16], U16, name="offsets")
+        nc.sync.dma_start(offsets[:], offs)
+
+        ts_raw = sb("ts_raw", [P, T], U8)
+        us_raw = sb("us_raw", [P, 2, R], U8)
+        ds_raw = sb("ds_raw", [P, 2, N], U8)
+        for q in range(4):
+            nc.sync.dma_start(
+                ts_raw[QUAD * q + 24 : QUAD * q + 32, :].bitcast(I32), tab_scales[:, 4 * q : 4 * q + 4, :].bitcast(I32)
+            )
+        for raw, scales in ((us_raw, wu_scales), (ds_raw, wd_scales)):
+            nc.gpsimd.memset(raw[:].bitcast(I32), 0)
+            for q in range(4):
+                nc.gpsimd.dma_start(
+                    raw[QUAD * q : QUAD * q + 4].bitcast(I32),
+                    scales[:, 4 * q : 4 * q + 4, :].rearrange("a r n -> r a n").bitcast(I32),
+                )
+        for q in range(4):
+            nc.vector.memset(ts_raw[QUAD * q : QUAD * q + 24, :].bitcast(I32), 0)
+
+        tab_raw = sb("tab_raw", [P, T], I32, tag="stream2")
+        nc.sync.dma_start(tab_raw[:], tab_words[0].rearrange("p t i -> p (t i)").bitcast(I32))
+
+        wg_raw = {}
+
+        def load_wg(a, b):
+            wg_raw[a, b] = sb(f"wg_raw{a}{b}", [P, PACK, PASS], F32, tag=f"stream{a}")
+            rows = wg[PASS * a : PASS * (a + 1), PASS * b : PASS * (b + 1)]
+            nc.sync.dma_start(wg_raw[a, b][:], rows.rearrange("(p j) c -> p j c", j=PACK))
+
+        wu_raw = {}
+
+        def load_wu(b):
+            wu_raw[b] = sb(f"wu_raw{b}", [P, 2, PASS], I32, tag="wu_raw")
+            words = wu_words.rearrange("a p r i -> p a (r i)")
+            nc.sync.dma_start(wu_raw[b][:], words[:, :, 4 * PASS * b : 4 * PASS * (b + 1)].bitcast(I32))
+
+        gate_raw = {}
+
+        def load_gate(t, tag):
+            gate_raw[t] = sb(f"gate_raw{t}", [P, T], F32, tag=tag)
+            nc.sync.dma_start(gate_raw[t][:], gT.rearrange("(p t) c -> p t c", t=PACK)[:, t, :])
+
+        load_wg(0, 0)
+        load_wg(1, 0)
+        load_wu(0)
+
+        ts_picked = sb("ts_picked", [P, J], U8)
+        nc.vector.tensor_copy(ts_picked[:], ts_raw[:].indirect(offsets[:]))
+        tab_scale = []
+        for a in range(2):
+            plane = sb(f"tab_scale{a}", [P, J], U8)
+            first = 24 + 4 * a
+            nc.scalar.dma_start(plane[0 : P - first, :].bitcast(I32), ts_picked[first:P, :].bitcast(I32))
+            tab_scale.append(plane)
+
+        wgo_sb = sb("wgo_sb", [P, J], F32, tag="ts_raw")
+        nc.sync.dma_start(wgo_sb[:], wgo)
+        tab_picked = sb("tab_picked", [P, J], I32)
+        nc.vector.tensor_copy(tab_picked[:].bitcast(U32), tab_raw[:].bitcast(U32).indirect(offsets[:]))
+        tab_codes = sb("tab_codes", [P, 2, 2 * J], U8)
+        nc.vector.tensor_copy(
+            tab_codes[:].bitcast(U16), tab_picked[:].bitcast(U16).rearrange("p (j d) -> p d j", d=2)
+        )
+        load_gate(0, "stream2")
+        wd_raw = sb("wd_raw", [P, 2, 2 * N], U8, tag="ts_picked")
+        nc.sync.dma_start(wd_raw[:].bitcast(I32), wd_words.rearrange("a p n -> p a n").bitcast(I32))
+
+        wu_scale = sb("wu_scale", [P, 2, R], U8)
+        nc.vector.tensor_copy(
+            wu_scale[:].rearrange("p a (b t m) -> p (a b) m t", b=2, t=PACK),
+            us_raw[:].rearrange("p a (b m t) -> p (a b) m t", b=2, t=PACK),
+        )
+
+        wu_codes = {}
+
+        def deal_wu(b):
+            wu_codes[b] = sb(f"wu_codes{b}", [P, 2, PASS], I32)
+            nc.vector.tensor_copy(
+                wu_codes[b][:].rearrange("p a (t m) -> p a m t", t=PACK),
+                wu_raw[b][:].rearrange("p a (m t) -> p a m t", t=PACK),
+            )
+
+        wg_codes, wg_scale = {}, {}
+
+        def quantise_wg(a, b):
+            rounded = sb(f"wg_bf{a}{b}", [P, PACK * PASS], BF16, tag=f"bf{a}{b}")
+            dst = rounded[:].rearrange("p (t m j) -> p m j t", t=PACK, j=PACK)
+            src = wg_raw[a, b][:].rearrange("p j (m t) -> p m j t", t=PACK)
+            for m0 in range(0, P, P // 2):
+                if (a, b) == (1, 0) and m0:
+                    nc.vector.tensor_copy(dst[:, m0 : m0 + P // 2], src[:, m0 : m0 + P // 2])
+                else:
+                    nc.scalar.copy(dst[:, m0 : m0 + P // 2], src[:, m0 : m0 + P // 2])
+            wg_codes[a, b] = sb(f"wg_codes{a}{b}", [P, PASS], U32)
+            wg_scale[a, b] = sb(f"wg_scale{a}{b}", [P, PASS], U8)
+            nc.vector.quantize_mx(out=wg_codes[a, b][:].bitcast(FP8X4), scales=wg_scale[a, b][:], in_=rounded[:])
+
+        gate = {}
+
+        def gather_gate(t, tag=None):
+            gate[t] = sb(f"gate{t}", [P, J], F32, tag=tag)
+            nc.vector.tensor_tensor(gate[t][:], gate_raw[t][:].indirect(offsets[:]), wgo_sb[:], MULT)
+
+        h_codes, h_scale = {}, {}
+
+        def hidden(b, half):
+            rounded = sb(f"h_bf{b}{half}", [P, PACK * HALF], BF16, tag=f"h_bf{b}{half}")
+            for s in range(HALF // P):
+                j0 = HALF * half + P * s
+                ga = psum.tile([P, PACK * P], F32, name="ga", tag="ga", bufs=3)
+                ub = psum.tile([P, PACK * P], F32, name="ub", tag="ub", bufs=3)
+                for t in range(PACK):
+                    for a in range(2):
+                        nc.tensor.matmul_mx(
+                            out=ga[:, P * t : P * (t + 1)],
+                            lhsT=wg_codes[a, b][:, P * t : P * (t + 1)].bitcast(FP8X4),
+                            lhsT_scale=wg_scale[a, b][:, P * t : P * (t + 1)],
+                            rhs=tab_codes[:, a, 2 * j0 : 2 * (j0 + P)].bitcast(FP4X4),
+                            rhs_scale=tab_scale[a][:, j0 : j0 + P],
+                            start=(a == 0),
+                            stop=(a == 1),
+                        )
+                for t in range(PACK):
+                    for a in range(2):
+                        nc.tensor.matmul_mx(
+                            out=ub[:, P * t : P * (t + 1)],
+                            lhsT=wu_codes[b][:, a, P * t : P * (t + 1)].bitcast(FP8X4),
+                            lhsT_scale=wu_scale[:, a, PASS * b + P * t : PASS * b + P * (t + 1)],
+                            rhs=tab_codes[:, a, 2 * j0 : 2 * (j0 + P)].bitcast(FP4X4),
+                            rhs_scale=tab_scale[a][:, j0 : j0 + P],
+                            start=(a == 0),
+                            stop=(a == 1),
+                        )
+                act = ring.tile([P, P, PACK], F32, name="act")
+                nc.scalar.activation(act[:], ga[:].rearrange("p (t n) -> p n t", t=PACK), SILU)
+                nc.vector.tensor_tensor(
+                    rounded[:, PACK * P * s : PACK * P * (s + 1)].rearrange("p (n t) -> p n t", t=PACK),
+                    ub[:].rearrange("p (t n) -> p n t", t=PACK),
+                    act[:],
+                    MULT,
+                )
+            h_codes[b, half] = sb(f"h_codes{b}{half}", [P, HALF], U32)
+            h_scale[b, half] = sb(f"h_scale{b}{half}", [P, HALF], U8)
+            nc.vector.quantize_mx(out=h_codes[b, half][:].bitcast(FP8X4), scales=h_scale[b, half][:], in_=rounded[:])
+
+        y_sb = [sb(f"y_sb{t}", [P, J], F32) for t in range(PACK)]
+
+        def down(t, half):
+            y = psum.tile([P, HALF], F32, name="y", tag="y", bufs=2)
+            for a in range(2):
+                nc.tensor.matmul_mx(
+                    out=y[:],
+                    lhsT=wd_codes[:, a, 2 * P * t : 2 * P * (t + 1)].bitcast(FP4X4),
+                    lhsT_scale=wd_scale[:, a, P * t : P * (t + 1)],
+                    rhs=h_codes[a, half][:].bitcast(FP8X4),
+                    rhs_scale=h_scale[a, half][:],
+                    start=(a == 0),
+                    stop=(a == 1),
+                )
+            nc.scalar.copy(y_sb[t][:, HALF * half : HALF * (half + 1)], y[:])
+
+        page = {}
+
+        def clear(t, engine, tag=None):
+            page[t] = sb(f"page{t}", [P, T], F32, tag=tag)
+            for c0 in range(0, T, PIECE):
+                engine.memset(page[t][:, c0 : c0 + PIECE], 0.0)
+
+        def scatter(t, j0, j1):
+            nc.vector.tensor_tensor(
+                page[t][:].indirect(offsets[:, j0 // 16 : j1 // 16]), y_sb[t][:, j0:j1], gate[t][:, j0:j1], MULT
+            )
+
+        deal_wu(0)
+        load_wu(1)
+        quantise_wg(0, 0)
+        load_wg(0, 1)
+        quantise_wg(1, 0)
+        load_wg(1, 1)
+        clear(0, nc.gpsimd, tag="bf00")
+        clear(2, nc.gpsimd, tag="bf10")
+        hidden(0, 0)
+        gather_gate(0)
+        load_gate(1, "stream2")
+        hidden(0, 1)
+        quantise_wg(0, 1)
+        load_gate(2, "stream0")
+        quantise_wg(1, 1)
+        load_gate(3, "stream1")
+        clear(3, nc.gpsimd, tag="bf01")
+        deal_wu(1)
+        wd_scale = sb("wd_scale", [P, 2, N], U8)
+        nc.vector.tensor_copy(
+            wd_scale[:].rearrange("p a (t m) -> p a m t", t=PACK), ds_raw[:].rearrange("p a (m t) -> p a m t", t=PACK)
+        )
+        wd_codes = sb("wd_codes", [P, 2, 2 * N], U8)
+        nc.vector.tensor_copy(
+            wd_codes[:].bitcast(U16).rearrange("p a (t m) -> p a m t", t=PACK),
+            wd_raw[:].bitcast(U16).rearrange("p a (m t) -> p a m t", t=PACK),
+        )
+        gather_gate(1)
+        hidden(1, 0)
+        gather_gate(2)
+        down(0, 0)
+        scatter(0, 0, HALF)
+        hidden(1, 1)
+        gather_gate(3, tag="h_bf11")
+        down(0, 1)
+        for t in range(1, PACK):
+            down(t, 0)
+            down(t, 1)
+        page[1] = sb("page1", [P, T], F32)
+        nc.vector.memset(page[1][:], 0.0)
+
+        pieces = T // PIECE
+        out_bf = [sb(f"out_bf{u}", [P, PIECE, PACK], BF16) for u in range(pieces)]
+        out_rows = out_0.rearrange("(p t) c -> p t c", t=PACK)
+        for t in range(PACK):
+            scatter(t, HALF if t == 0 else 0, J)
+            nc.sync.dma_start(out_rows[:, t, :], page[t][:])
+            for u in range(pieces):
+                src = page[t][:, PIECE * u : PIECE * (u + 1)]
+                if t == PACK - 1 and u < pieces // 2:
+                    nc.vector.tensor_copy(out_bf[u][:, :, t], src)
+                elif t == PACK - 2 and u < pieces // 2:
+                    nc.scalar.copy(out_bf[u][:, :, t : t + 2], src.unsqueeze(2).to_broadcast([P, PIECE, 2]))
+                else:
+                    nc.scalar.copy(out_bf[u][:, :, t], src)
+
+        out_scale = sb("out_scale", [P, T], U8)
+        out_words = out_1[0].rearrange("p t i -> p (t i)").bitcast(I32)
+        for u in range(pieces):
+            codes = sb(f"out_codes{u}", [P, PIECE], I32)
+            nc.vector.quantize_mx(
+                out=codes[:].bitcast(FP8X4),
+                scales=out_scale[:, PIECE * u : PIECE * (u + 1)],
+                in_=out_bf[u][:].rearrange("p c t -> p (c t)"),
+            )
+            nc.sync.dma_start(out_words[:, PIECE * u : PIECE * (u + 1)], codes[:])
+        for q in range(4):
+            queue = nc.scalar if q % 2 else nc.sync
+            queue.dma_start(
+                out_2[0, 4 * q : 4 * q + 4, :].bitcast(I32), out_scale[QUAD * q : QUAD * q + 4, :].bitcast(I32)
+            )

@@ -41,18 +41,20 @@ def tile_list_modp_gsilu_gateP_kernel(
 
         ts_raw = sb("ts_raw", [P, T], U8)
         us_raw = sb("us_raw", [P, 2, R], U8)
-        ds_raw = sb("ds_raw", [P, 2, N], U8)
         for q in range(4):
             nc.sync.dma_start(
                 ts_raw[QUAD * q + 24 : QUAD * q + 32, :].bitcast(I32), tab_scales[:, 4 * q : 4 * q + 4, :].bitcast(I32)
             )
-        for raw, scales in ((us_raw, wu_scales), (ds_raw, wd_scales)):
-            nc.gpsimd.memset(raw[:].bitcast(I32), 0)
+
+        def load_weight_scales(raw, scales, queue):
+            nc.vector.memset(raw[:].bitcast(I32), 0)
             for q in range(4):
-                nc.gpsimd.dma_start(
+                queue.dma_start(
                     raw[QUAD * q : QUAD * q + 4].bitcast(I32),
                     scales[:, 4 * q : 4 * q + 4, :].rearrange("a r n -> r a n").bitcast(I32),
                 )
+
+        load_weight_scales(us_raw, wu_scales, nc.scalar)
         for q in range(4):
             nc.vector.memset(ts_raw[QUAD * q : QUAD * q + 24, :].bitcast(I32), 0)
 
@@ -106,9 +108,11 @@ def tile_list_modp_gsilu_gateP_kernel(
 
         wu_scale = sb("wu_scale", [P, 2, R], U8)
         nc.vector.tensor_copy(
-            wu_scale[:].rearrange("p a (b t m) -> p (a b) m t", b=2, t=PACK),
-            us_raw[:].rearrange("p a (b m t) -> p (a b) m t", b=2, t=PACK),
+            wu_scale[:].rearrange("p a (b t m) -> p (a b) t m", b=2, t=PACK),
+            us_raw[:].rearrange("p a (b m t) -> p (a b) t m", b=2, t=PACK),
         )
+        ds_raw = sb("ds_raw", [P, 2, N], U8, tag="us_raw")
+        load_weight_scales(ds_raw, wd_scales, nc.sync)
 
         wu_codes = {}
 
@@ -122,14 +126,11 @@ def tile_list_modp_gsilu_gateP_kernel(
         wg_codes, wg_scale = {}, {}
 
         def quantise_wg(a, b):
-            rounded = sb(f"wg_bf{a}{b}", [P, PACK * PASS], BF16, tag=f"bf{a}{b}")
+            rounded = sb(f"wg_bf{a}{b}", [P, PACK * PASS], BF16)
             dst = rounded[:].rearrange("p (t m j) -> p m j t", t=PACK, j=PACK)
             src = wg_raw[a, b][:].rearrange("p j (m t) -> p m j t", t=PACK)
             for m0 in range(0, P, P // 2):
-                if (a, b) == (1, 0) and m0:
-                    nc.vector.tensor_copy(dst[:, m0 : m0 + P // 2], src[:, m0 : m0 + P // 2])
-                else:
-                    nc.scalar.copy(dst[:, m0 : m0 + P // 2], src[:, m0 : m0 + P // 2])
+                nc.scalar.copy(dst[:, m0 : m0 + P // 2], src[:, m0 : m0 + P // 2])
             wg_codes[a, b] = sb(f"wg_codes{a}{b}", [P, PASS], U32)
             wg_scale[a, b] = sb(f"wg_scale{a}{b}", [P, PASS], U8)
             nc.vector.quantize_mx(out=wg_codes[a, b][:].bitcast(FP8X4), scales=wg_scale[a, b][:], in_=rounded[:])
@@ -198,12 +199,7 @@ def tile_list_modp_gsilu_gateP_kernel(
                 )
             nc.scalar.copy(y_sb[t][:, HALF * half : HALF * (half + 1)], y[:])
 
-        page = {}
-
-        def clear(t, engine, tag=None):
-            page[t] = sb(f"page{t}", [P, T], F32, tag=tag)
-            for c0 in range(0, T, PIECE):
-                engine.memset(page[t][:, c0 : c0 + PIECE], 0.0)
+        page = [sb(f"page{t}", [P, T], F32) for t in range(PACK)]
 
         def scatter(t, j0, j1):
             nc.vector.tensor_tensor(
@@ -216,8 +212,6 @@ def tile_list_modp_gsilu_gateP_kernel(
         load_wg(0, 1)
         quantise_wg(1, 0)
         load_wg(1, 1)
-        clear(0, nc.gpsimd, tag="bf00")
-        clear(2, nc.gpsimd, tag="bf10")
         hidden(0, 0)
         gather_gate(0)
         load_gate(1, "stream2")
@@ -226,11 +220,10 @@ def tile_list_modp_gsilu_gateP_kernel(
         load_gate(2, "stream0")
         quantise_wg(1, 1)
         load_gate(3, "stream1")
-        clear(3, nc.gpsimd, tag="bf01")
         deal_wu(1)
         wd_scale = sb("wd_scale", [P, 2, N], U8)
         nc.vector.tensor_copy(
-            wd_scale[:].rearrange("p a (t m) -> p a m t", t=PACK), ds_raw[:].rearrange("p a (m t) -> p a m t", t=PACK)
+            wd_scale[:].rearrange("p a (t m) -> p a t m", t=PACK), ds_raw[:].rearrange("p a (m t) -> p a t m", t=PACK)
         )
         wd_codes = sb("wd_codes", [P, 2, 2 * N], U8)
         nc.vector.tensor_copy(
@@ -239,22 +232,23 @@ def tile_list_modp_gsilu_gateP_kernel(
         )
         gather_gate(1)
         hidden(1, 0)
-        gather_gate(2)
+        for t in range(PACK):
+            nc.vector.memset(page[t][:], 0.0)
         down(0, 0)
         scatter(0, 0, HALF)
         hidden(1, 1)
-        gather_gate(3, tag="h_bf11")
+        gather_gate(2, tag="h_bf11")
         down(0, 1)
         for t in range(1, PACK):
             down(t, 0)
             down(t, 1)
-        page[1] = sb("page1", [P, T], F32)
-        nc.vector.memset(page[1][:], 0.0)
 
         pieces = T // PIECE
         out_bf = [sb(f"out_bf{u}", [P, PIECE, PACK], BF16) for u in range(pieces)]
         out_rows = out_0.rearrange("(p t) c -> p t c", t=PACK)
         for t in range(PACK):
+            if t == PACK - 1:
+                gather_gate(t, tag="h_bf11")
             scatter(t, HALF if t == 0 else 0, J)
             nc.sync.dma_start(out_rows[:, t, :], page[t][:])
             for u in range(pieces):

@@ -21,7 +21,8 @@ PACK = 4
 PASS = P * PACK
 QUAD = 32
 HALF = J // 2
-PIECE = 512
+EDGES = (0, 512, 768, 1280, 1792, 2048)
+VECTOR_PIECES = 2
 
 
 def tile_list_modp_gsilu_gateP_kernel(
@@ -30,89 +31,82 @@ def tile_list_modp_gsilu_gateP_kernel(
     nc = tc.nc
     with ExitStack() as ctx:
         keep = ctx.enter_context(tc.tile_pool(name="keep", bufs=1))
+        shared = ctx.enter_context(tc.tile_pool(name="shared", bufs=1))
         ring = ctx.enter_context(tc.tile_pool(name="ring", bufs=3))
         psum = ctx.enter_context(tc.psum_pool(name="psum", bufs=1))
 
         def sb(name, shape, dtype, tag=None):
             return keep.tile(shape, dtype, name=name, tag=tag or name, align_bytes=64)
 
+        def staged(name, shape, dtype, kib):
+            return shared.tile(shape, dtype, name=name, offset=1024 * kib)
+
         offsets = keep.tile([P, J // 16], U16, name="offsets")
         nc.sync.dma_start(offsets[:], offs)
 
-        ts_raw = sb("ts_raw", [P, T], U8)
-        us_raw = sb("us_raw", [P, 2, R], U8)
-        for q in range(4):
-            nc.sync.dma_start(
-                ts_raw[QUAD * q + 24 : QUAD * q + 32, :].bitcast(I32), tab_scales[:, 4 * q : 4 * q + 4, :].bitcast(I32)
-            )
+        ts_raw = staged("ts_raw", [P, T], U8, 7)
+        ws_raw = sb("ws_raw", [P, R], U8)
+        nc.sync.dma_start(ts_raw[96:128, :].bitcast(I32), tab_scales.rearrange("a q t -> q a t").bitcast(I32))
+        nc.sync.dma_start(ws_raw[96:128, :].bitcast(I32), wu_scales.rearrange("a q r -> q a r").bitcast(I32))
+        nc.sync.dma_start(ws_raw[64:96, 0:N].bitcast(I32), wd_scales.rearrange("a q n -> q a n").bitcast(I32))
+        nc.vector.memset(ws_raw[0:64, :].bitcast(I32), 0)
+        nc.vector.memset(ws_raw[64:96, N:R].bitcast(I32), 0)
+        nc.vector.memset(ts_raw[0:96, :].bitcast(I32), 0)
 
-        def load_weight_scales(raw, scales, queue):
-            nc.vector.memset(raw[:].bitcast(I32), 0)
+        def place_scale_rows(queue, planes, rows):
             for q in range(4):
-                queue.dma_start(
-                    raw[QUAD * q : QUAD * q + 4].bitcast(I32),
-                    scales[:, 4 * q : 4 * q + 4, :].rearrange("a r n -> r a n").bitcast(I32),
-                )
+                queue.dma_start(planes[QUAD * q : QUAD * q + 4].bitcast(I32), rows[8 * q : 8 * (q + 1)].bitcast(I32))
 
-        load_weight_scales(us_raw, wu_scales, nc.scalar)
-        for q in range(4):
-            nc.vector.memset(ts_raw[QUAD * q : QUAD * q + 24, :].bitcast(I32), 0)
-
-        tab_raw = sb("tab_raw", [P, T], I32, tag="stream2")
+        tab_raw = staged("tab_raw", [P, T], I32, 12)
         nc.sync.dma_start(tab_raw[:], tab_words[0].rearrange("p t i -> p (t i)").bitcast(I32))
 
         wg_raw = {}
 
-        def load_wg(a, b):
-            wg_raw[a, b] = sb(f"wg_raw{a}{b}", [P, PACK, PASS], F32, tag=f"stream{a}")
+        def load_wg(a, b, kib):
+            wg_raw[a, b] = staged(f"wg_raw{a}{b}", [P, PACK, PASS], F32, kib)
             rows = wg[PASS * a : PASS * (a + 1), PASS * b : PASS * (b + 1)]
             nc.sync.dma_start(wg_raw[a, b][:], rows.rearrange("(p j) c -> p j c", j=PACK))
 
         wu_raw = {}
 
         def load_wu(b):
-            wu_raw[b] = sb(f"wu_raw{b}", [P, 2, PASS], I32, tag="wu_raw")
+            wu_raw[b] = staged(f"wu_raw{b}", [P, 2, PASS], I32, 8)
             words = wu_words.rearrange("a p r i -> p a (r i)")
             nc.sync.dma_start(wu_raw[b][:], words[:, :, 4 * PASS * b : 4 * PASS * (b + 1)].bitcast(I32))
 
         gate_raw = {}
 
-        def load_gate(t, tag):
-            gate_raw[t] = sb(f"gate_raw{t}", [P, T], F32, tag=tag)
+        def load_gate(t, kib):
+            gate_raw[t] = staged(f"gate_raw{t}", [P, T], F32, kib)
             nc.sync.dma_start(gate_raw[t][:], gT.rearrange("(p t) c -> p t c", t=PACK)[:, t, :])
 
-        load_wg(0, 0)
-        load_wg(1, 0)
-        load_wu(0)
+        load_wg(0, 0, 32)
+
+        ws_dealt = sb("ws_dealt", [P, R], U8)
+        nc.vector.tensor_copy(
+            ws_dealt[:].rearrange("p (b t m) -> p b t m", b=2, t=PACK),
+            ws_raw[:].rearrange("p (b m t) -> p b t m", b=2, t=PACK),
+        )
+        wu_scale = sb("wu_scale", [P, 2, R], U8)
+        place_scale_rows(nc.scalar, wu_scale, ws_dealt[96:128, :])
 
         ts_picked = sb("ts_picked", [P, J], U8)
         nc.vector.tensor_copy(ts_picked[:], ts_raw[:].indirect(offsets[:]))
-        tab_scale = []
-        for a in range(2):
-            plane = sb(f"tab_scale{a}", [P, J], U8)
-            first = 24 + 4 * a
-            nc.scalar.dma_start(plane[0 : P - first, :].bitcast(I32), ts_picked[first:P, :].bitcast(I32))
-            tab_scale.append(plane)
+        tab_scale = sb("tab_scale", [P, 2, J], U8)
+        place_scale_rows(nc.scalar, tab_scale, ts_picked[96:128, :])
+        load_wg(1, 0, 0)
+        load_wu(0)
 
-        wgo_sb = sb("wgo_sb", [P, J], F32, tag="ts_raw")
-        nc.sync.dma_start(wgo_sb[:], wgo)
-        tab_picked = sb("tab_picked", [P, J], I32)
+        tab_picked = staged("tab_picked", [P, J], I32, 24)
         nc.vector.tensor_copy(tab_picked[:].bitcast(U32), tab_raw[:].bitcast(U32).indirect(offsets[:]))
+        wgo_sb = staged("wgo_sb", [P, J], F32, 12)
+        nc.sync.dma_start(wgo_sb[:], wgo)
+        load_gate(0, 16)
         tab_codes = sb("tab_codes", [P, 2, 2 * J], U8)
         nc.vector.tensor_copy(
             tab_codes[:].bitcast(U16), tab_picked[:].bitcast(U16).rearrange("p (j d) -> p d j", d=2)
         )
-        load_gate(0, "stream2")
-        wd_raw = sb("wd_raw", [P, 2, 2 * N], U8, tag="ts_picked")
-        nc.sync.dma_start(wd_raw[:].bitcast(I32), wd_words.rearrange("a p n -> p a n").bitcast(I32))
-
-        wu_scale = sb("wu_scale", [P, 2, R], U8)
-        nc.vector.tensor_copy(
-            wu_scale[:].rearrange("p a (b t m) -> p (a b) t m", b=2, t=PACK),
-            us_raw[:].rearrange("p a (b m t) -> p (a b) t m", b=2, t=PACK),
-        )
-        ds_raw = sb("ds_raw", [P, 2, N], U8, tag="us_raw")
-        load_weight_scales(ds_raw, wd_scales, nc.sync)
+        load_wg(0, 1, 24)
 
         wu_codes = {}
 
@@ -156,7 +150,7 @@ def tile_list_modp_gsilu_gateP_kernel(
                             lhsT=wg_codes[a, b][:, P * t : P * (t + 1)].bitcast(FP8X4),
                             lhsT_scale=wg_scale[a, b][:, P * t : P * (t + 1)],
                             rhs=tab_codes[:, a, 2 * j0 : 2 * (j0 + P)].bitcast(FP4X4),
-                            rhs_scale=tab_scale[a][:, j0 : j0 + P],
+                            rhs_scale=tab_scale[:, a, j0 : j0 + P],
                             start=(a == 0),
                             stop=(a == 1),
                         )
@@ -167,7 +161,7 @@ def tile_list_modp_gsilu_gateP_kernel(
                             lhsT=wu_codes[b][:, a, P * t : P * (t + 1)].bitcast(FP8X4),
                             lhsT_scale=wu_scale[:, a, PASS * b + P * t : PASS * b + P * (t + 1)],
                             rhs=tab_codes[:, a, 2 * j0 : 2 * (j0 + P)].bitcast(FP4X4),
-                            rhs_scale=tab_scale[a][:, j0 : j0 + P],
+                            rhs_scale=tab_scale[:, a, j0 : j0 + P],
                             start=(a == 0),
                             stop=(a == 1),
                         )
@@ -209,22 +203,21 @@ def tile_list_modp_gsilu_gateP_kernel(
         deal_wu(0)
         load_wu(1)
         quantise_wg(0, 0)
-        load_wg(0, 1)
+        load_wg(1, 1, 32)
+        wd_scale = sb("wd_scale", [P, 2, N], U8, tag="wg_bf00")
+        place_scale_rows(nc.sync, wd_scale, ws_dealt[64:96, 0:N])
         quantise_wg(1, 0)
-        load_wg(1, 1)
+        load_gate(1, 0)
+        wd_raw = sb("wd_raw", [P, 2, 2 * N], U8, tag="wg_bf10")
+        nc.sync.dma_start(wd_raw[:].bitcast(I32), wd_words.rearrange("a p n -> p a n").bitcast(I32))
         hidden(0, 0)
         gather_gate(0)
-        load_gate(1, "stream2")
         hidden(0, 1)
         quantise_wg(0, 1)
-        load_gate(2, "stream0")
+        load_gate(2, 24)
         quantise_wg(1, 1)
-        load_gate(3, "stream1")
+        load_gate(3, 32)
         deal_wu(1)
-        wd_scale = sb("wd_scale", [P, 2, N], U8)
-        nc.vector.tensor_copy(
-            wd_scale[:].rearrange("p a (t m) -> p a t m", t=PACK), ds_raw[:].rearrange("p a (m t) -> p a t m", t=PACK)
-        )
         wd_codes = sb("wd_codes", [P, 2, 2 * N], U8)
         nc.vector.tensor_copy(
             wd_codes[:].bitcast(U16).rearrange("p a (t m) -> p a m t", t=PACK),
@@ -243,33 +236,33 @@ def tile_list_modp_gsilu_gateP_kernel(
             down(t, 0)
             down(t, 1)
 
-        pieces = T // PIECE
-        out_bf = [sb(f"out_bf{u}", [P, PIECE, PACK], BF16) for u in range(pieces)]
+        pieces = list(zip(EDGES[:-1], EDGES[1:]))
+        out_bf = [sb(f"out_bf{c0}", [P, c1 - c0, PACK], BF16) for c0, c1 in pieces]
         out_rows = out_0.rearrange("(p t) c -> p t c", t=PACK)
         for t in range(PACK):
             if t == PACK - 1:
                 gather_gate(t, tag="h_bf11")
             scatter(t, HALF if t == 0 else 0, J)
             nc.sync.dma_start(out_rows[:, t, :], page[t][:])
-            for u in range(pieces):
-                src = page[t][:, PIECE * u : PIECE * (u + 1)]
-                if t == PACK - 1 and u < pieces // 2:
+            for u, (c0, c1) in enumerate(pieces):
+                src = page[t][:, c0:c1]
+                if t == PACK - 1 and u < VECTOR_PIECES:
                     nc.vector.tensor_copy(out_bf[u][:, :, t], src)
-                elif t == PACK - 2 and u < pieces // 2:
-                    nc.scalar.copy(out_bf[u][:, :, t : t + 2], src.unsqueeze(2).to_broadcast([P, PIECE, 2]))
+                elif t == PACK - 2 and u < VECTOR_PIECES:
+                    nc.scalar.copy(out_bf[u][:, :, t : t + 2], src.unsqueeze(2).to_broadcast([P, c1 - c0, 2]))
                 else:
                     nc.scalar.copy(out_bf[u][:, :, t], src)
 
         out_scale = sb("out_scale", [P, T], U8)
         out_words = out_1[0].rearrange("p t i -> p (t i)").bitcast(I32)
-        for u in range(pieces):
-            codes = sb(f"out_codes{u}", [P, PIECE], I32)
+        for u, (c0, c1) in enumerate(pieces):
+            codes = sb(f"out_codes{u}", [P, c1 - c0], I32)
             nc.vector.quantize_mx(
                 out=codes[:].bitcast(FP8X4),
-                scales=out_scale[:, PIECE * u : PIECE * (u + 1)],
+                scales=out_scale[:, c0:c1],
                 in_=out_bf[u][:].rearrange("p c t -> p (c t)"),
             )
-            nc.sync.dma_start(out_words[:, PIECE * u : PIECE * (u + 1)], codes[:])
+            nc.sync.dma_start(out_words[:, c0:c1], codes[:])
         for q in range(4):
             queue = nc.scalar if q % 2 else nc.sync
             queue.dma_start(

@@ -19,10 +19,19 @@ SILU = mybir.ActivationFunctionType.Silu
 P = 128
 PACK = 4
 PASS = P * PACK
+PASSES = 2
 QUAD = 32
 HALF = J // 2
+GROUP = 16
+
 EDGES = (0, 512, 768, 1280, 1792, 2048)
 VECTOR_PIECES = 2
+
+AT_WG10, AT_TAB_SCALES, AT_WU = 0, 7, 8
+AT_TAB_WORDS, AT_WGO, AT_GATE0 = 12, 12, 16
+AT_PICKED, AT_WG01 = 24, 24
+AT_WG00, AT_WG11 = 32, 32
+AT_GATE1, AT_GATE2, AT_GATE3 = AT_WG10, AT_WG01, AT_WG11
 
 
 def tile_list_modp_gsilu_gateP_kernel(
@@ -41,10 +50,10 @@ def tile_list_modp_gsilu_gateP_kernel(
         def staged(name, shape, dtype, kib):
             return shared.tile(shape, dtype, name=name, offset=1024 * kib)
 
-        offsets = keep.tile([P, J // 16], U16, name="offsets")
+        offsets = keep.tile([P, J // GROUP], U16, name="offsets")
         nc.sync.dma_start(offsets[:], offs)
 
-        ts_raw = staged("ts_raw", [P, T], U8, 7)
+        ts_raw = staged("ts_raw", [P, T], U8, AT_TAB_SCALES)
         ws_raw = sb("ws_raw", [P, R], U8)
         nc.sync.dma_start(ts_raw[96:128, :].bitcast(I32), tab_scales.rearrange("a q t -> q a t").bitcast(I32))
         nc.sync.dma_start(ws_raw[96:128, :].bitcast(I32), wu_scales.rearrange("a q r -> q a r").bitcast(I32))
@@ -53,11 +62,13 @@ def tile_list_modp_gsilu_gateP_kernel(
         nc.vector.memset(ws_raw[64:96, N:R].bitcast(I32), 0)
         nc.vector.memset(ts_raw[0:96, :].bitcast(I32), 0)
 
-        def place_scale_rows(queue, planes, rows):
-            for q in range(4):
-                queue.dma_start(planes[QUAD * q : QUAD * q + 4].bitcast(I32), rows[8 * q : 8 * (q + 1)].bitcast(I32))
+        def place_scale_rows(queue, scale, rows):
+            for quad in range(P // QUAD):
+                queue.dma_start(
+                    scale[QUAD * quad : QUAD * quad + 4].bitcast(I32), rows[8 * quad : 8 * (quad + 1)].bitcast(I32)
+                )
 
-        tab_raw = staged("tab_raw", [P, T], I32, 12)
+        tab_raw = staged("tab_raw", [P, T], I32, AT_TAB_WORDS)
         nc.sync.dma_start(tab_raw[:], tab_words[0].rearrange("p t i -> p (t i)").bitcast(I32))
 
         wg_raw = {}
@@ -65,14 +76,14 @@ def tile_list_modp_gsilu_gateP_kernel(
         def load_wg(a, b, kib):
             wg_raw[a, b] = staged(f"wg_raw{a}{b}", [P, PACK, PASS], F32, kib)
             rows = wg[PASS * a : PASS * (a + 1), PASS * b : PASS * (b + 1)]
-            nc.sync.dma_start(wg_raw[a, b][:], rows.rearrange("(p j) c -> p j c", j=PACK))
+            nc.sync.dma_start(wg_raw[a, b][:], rows.rearrange("(p i) c -> p i c", i=PACK))
 
         wu_raw = {}
 
         def load_wu(b):
-            wu_raw[b] = staged(f"wu_raw{b}", [P, 2, PASS], I32, 8)
+            wu_raw[b] = staged(f"wu_raw{b}", [P, PASSES, PASS], I32, AT_WU)
             words = wu_words.rearrange("a p r i -> p a (r i)")
-            nc.sync.dma_start(wu_raw[b][:], words[:, :, 4 * PASS * b : 4 * PASS * (b + 1)].bitcast(I32))
+            nc.sync.dma_start(wu_raw[b][:], words[:, :, PACK * PASS * b : PACK * PASS * (b + 1)].bitcast(I32))
 
         gate_raw = {}
 
@@ -80,38 +91,38 @@ def tile_list_modp_gsilu_gateP_kernel(
             gate_raw[t] = staged(f"gate_raw{t}", [P, T], F32, kib)
             nc.sync.dma_start(gate_raw[t][:], gT.rearrange("(p t) c -> p t c", t=PACK)[:, t, :])
 
-        load_wg(0, 0, 32)
+        load_wg(0, 0, AT_WG00)
 
         ws_dealt = sb("ws_dealt", [P, R], U8)
         nc.vector.tensor_copy(
-            ws_dealt[:].rearrange("p (b t m) -> p b t m", b=2, t=PACK),
-            ws_raw[:].rearrange("p (b m t) -> p b t m", b=2, t=PACK),
+            ws_dealt[:].rearrange("p (b t m) -> p b t m", b=R // PASS, t=PACK),
+            ws_raw[:].rearrange("p (b m t) -> p b t m", b=R // PASS, t=PACK),
         )
-        wu_scale = sb("wu_scale", [P, 2, R], U8)
+        wu_scale = sb("wu_scale", [P, PASSES, R], U8)
         place_scale_rows(nc.scalar, wu_scale, ws_dealt[96:128, :])
 
         ts_picked = sb("ts_picked", [P, J], U8)
         nc.vector.tensor_copy(ts_picked[:], ts_raw[:].indirect(offsets[:]))
-        tab_scale = sb("tab_scale", [P, 2, J], U8)
+        tab_scale = sb("tab_scale", [P, PASSES, J], U8)
         place_scale_rows(nc.scalar, tab_scale, ts_picked[96:128, :])
-        load_wg(1, 0, 0)
+        load_wg(1, 0, AT_WG10)
         load_wu(0)
 
-        tab_picked = staged("tab_picked", [P, J], I32, 24)
+        tab_picked = staged("tab_picked", [P, J], I32, AT_PICKED)
         nc.vector.tensor_copy(tab_picked[:].bitcast(U32), tab_raw[:].bitcast(U32).indirect(offsets[:]))
-        wgo_sb = staged("wgo_sb", [P, J], F32, 12)
+        wgo_sb = staged("wgo_sb", [P, J], F32, AT_WGO)
         nc.sync.dma_start(wgo_sb[:], wgo)
-        load_gate(0, 16)
-        tab_codes = sb("tab_codes", [P, 2, 2 * J], U8)
+        load_gate(0, AT_GATE0)
+        tab_codes = sb("tab_codes", [P, PASSES, 2 * J], U8)
         nc.vector.tensor_copy(
-            tab_codes[:].bitcast(U16), tab_picked[:].bitcast(U16).rearrange("p (j d) -> p d j", d=2)
+            tab_codes[:].bitcast(U16), tab_picked[:].bitcast(U16).rearrange("p (j a) -> p a j", a=PASSES)
         )
-        load_wg(0, 1, 24)
+        load_wg(0, 1, AT_WG01)
 
         wu_codes = {}
 
         def deal_wu(b):
-            wu_codes[b] = sb(f"wu_codes{b}", [P, 2, PASS], I32)
+            wu_codes[b] = sb(f"wu_codes{b}", [P, PASSES, PASS], I32)
             nc.vector.tensor_copy(
                 wu_codes[b][:].rearrange("p a (t m) -> p a m t", t=PACK),
                 wu_raw[b][:].rearrange("p a (m t) -> p a m t", t=PACK),
@@ -121,8 +132,8 @@ def tile_list_modp_gsilu_gateP_kernel(
 
         def quantise_wg(a, b):
             rounded = sb(f"wg_bf{a}{b}", [P, PACK * PASS], BF16)
-            dst = rounded[:].rearrange("p (t m j) -> p m j t", t=PACK, j=PACK)
-            src = wg_raw[a, b][:].rearrange("p j (m t) -> p m j t", t=PACK)
+            dst = rounded[:].rearrange("p (t m i) -> p m i t", t=PACK, i=PACK)
+            src = wg_raw[a, b][:].rearrange("p i (m t) -> p m i t", t=PACK)
             for m0 in range(0, P, P // 2):
                 nc.scalar.copy(dst[:, m0 : m0 + P // 2], src[:, m0 : m0 + P // 2])
             wg_codes[a, b] = sb(f"wg_codes{a}{b}", [P, PASS], U32)
@@ -138,13 +149,13 @@ def tile_list_modp_gsilu_gateP_kernel(
         h_codes, h_scale = {}, {}
 
         def hidden(b, half):
-            rounded = sb(f"h_bf{b}{half}", [P, PACK * HALF], BF16, tag=f"h_bf{b}{half}")
+            rounded = sb(f"h_bf{b}{half}", [P, PACK * HALF], BF16)
             for s in range(HALF // P):
                 j0 = HALF * half + P * s
                 ga = psum.tile([P, PACK * P], F32, name="ga", tag="ga", bufs=3)
                 ub = psum.tile([P, PACK * P], F32, name="ub", tag="ub", bufs=3)
                 for t in range(PACK):
-                    for a in range(2):
+                    for a in range(PASSES):
                         nc.tensor.matmul_mx(
                             out=ga[:, P * t : P * (t + 1)],
                             lhsT=wg_codes[a, b][:, P * t : P * (t + 1)].bitcast(FP8X4),
@@ -152,10 +163,10 @@ def tile_list_modp_gsilu_gateP_kernel(
                             rhs=tab_codes[:, a, 2 * j0 : 2 * (j0 + P)].bitcast(FP4X4),
                             rhs_scale=tab_scale[:, a, j0 : j0 + P],
                             start=(a == 0),
-                            stop=(a == 1),
+                            stop=(a == PASSES - 1),
                         )
                 for t in range(PACK):
-                    for a in range(2):
+                    for a in range(PASSES):
                         nc.tensor.matmul_mx(
                             out=ub[:, P * t : P * (t + 1)],
                             lhsT=wu_codes[b][:, a, P * t : P * (t + 1)].bitcast(FP8X4),
@@ -163,13 +174,13 @@ def tile_list_modp_gsilu_gateP_kernel(
                             rhs=tab_codes[:, a, 2 * j0 : 2 * (j0 + P)].bitcast(FP4X4),
                             rhs_scale=tab_scale[:, a, j0 : j0 + P],
                             start=(a == 0),
-                            stop=(a == 1),
+                            stop=(a == PASSES - 1),
                         )
-                act = ring.tile([P, P, PACK], F32, name="act")
-                nc.scalar.activation(act[:], ga[:].rearrange("p (t n) -> p n t", t=PACK), SILU)
+                act = ring.tile([P, P // 2, PACK, 2], F32, name="act")
+                nc.scalar.activation(act[:], ga[:].rearrange("p (t c e) -> p c t e", t=PACK, e=2), SILU)
                 nc.vector.tensor_tensor(
-                    rounded[:, PACK * P * s : PACK * P * (s + 1)].rearrange("p (n t) -> p n t", t=PACK),
-                    ub[:].rearrange("p (t n) -> p n t", t=PACK),
+                    rounded[:, PACK * P * s : PACK * P * (s + 1)].rearrange("p (c e t) -> p c t e", t=PACK, e=2),
+                    ub[:].rearrange("p (t c e) -> p c t e", t=PACK, e=2),
                     act[:],
                     MULT,
                 )
@@ -181,7 +192,7 @@ def tile_list_modp_gsilu_gateP_kernel(
 
         def down(t, half):
             y = psum.tile([P, HALF], F32, name="y", tag="y", bufs=2)
-            for a in range(2):
+            for a in range(PASSES):
                 nc.tensor.matmul_mx(
                     out=y[:],
                     lhsT=wd_codes[:, a, 2 * P * t : 2 * P * (t + 1)].bitcast(FP4X4),
@@ -189,7 +200,7 @@ def tile_list_modp_gsilu_gateP_kernel(
                     rhs=h_codes[a, half][:].bitcast(FP8X4),
                     rhs_scale=h_scale[a, half][:],
                     start=(a == 0),
-                    stop=(a == 1),
+                    stop=(a == PASSES - 1),
                 )
             nc.scalar.copy(y_sb[t][:, HALF * half : HALF * (half + 1)], y[:])
 
@@ -197,28 +208,28 @@ def tile_list_modp_gsilu_gateP_kernel(
 
         def scatter(t, j0, j1):
             nc.vector.tensor_tensor(
-                page[t][:].indirect(offsets[:, j0 // 16 : j1 // 16]), y_sb[t][:, j0:j1], gate[t][:, j0:j1], MULT
+                page[t][:].indirect(offsets[:, j0 // GROUP : j1 // GROUP]), y_sb[t][:, j0:j1], gate[t][:, j0:j1], MULT
             )
 
         deal_wu(0)
         load_wu(1)
         quantise_wg(0, 0)
-        load_wg(1, 1, 32)
-        wd_scale = sb("wd_scale", [P, 2, N], U8, tag="wg_bf00")
+        load_wg(1, 1, AT_WG11)
+        wd_scale = sb("wd_scale", [P, PASSES, N], U8, tag="wg_bf00")
         place_scale_rows(nc.sync, wd_scale, ws_dealt[64:96, 0:N])
         quantise_wg(1, 0)
-        load_gate(1, 0)
-        wd_raw = sb("wd_raw", [P, 2, 2 * N], U8, tag="wg_bf10")
+        load_gate(1, AT_GATE1)
+        wd_raw = sb("wd_raw", [P, PASSES, 2 * N], U8, tag="wg_bf10")
         nc.sync.dma_start(wd_raw[:].bitcast(I32), wd_words.rearrange("a p n -> p a n").bitcast(I32))
         hidden(0, 0)
         gather_gate(0)
         hidden(0, 1)
         quantise_wg(0, 1)
-        load_gate(2, 24)
+        load_gate(2, AT_GATE2)
         quantise_wg(1, 1)
-        load_gate(3, 32)
+        load_gate(3, AT_GATE3)
         deal_wu(1)
-        wd_codes = sb("wd_codes", [P, 2, 2 * N], U8)
+        wd_codes = sb("wd_codes", [P, PASSES, 2 * N], U8)
         nc.vector.tensor_copy(
             wd_codes[:].bitcast(U16).rearrange("p a (t m) -> p a m t", t=PACK),
             wd_raw[:].bitcast(U16).rearrange("p a (m t) -> p a m t", t=PACK),
@@ -226,7 +237,7 @@ def tile_list_modp_gsilu_gateP_kernel(
         gather_gate(1)
         hidden(1, 0)
         for t in range(PACK):
-            nc.vector.memset(page[t][:], 0.0)
+            nc.vector.memset(page[t][:].bitcast(I32), 0)
         down(0, 0)
         scatter(0, 0, HALF)
         hidden(1, 1)
@@ -239,16 +250,17 @@ def tile_list_modp_gsilu_gateP_kernel(
         pieces = list(zip(EDGES[:-1], EDGES[1:]))
         out_bf = [sb(f"out_bf{c0}", [P, c1 - c0, PACK], BF16) for c0, c1 in pieces]
         out_rows = out_0.rearrange("(p t) c -> p t c", t=PACK)
+        last = PACK - 1
         for t in range(PACK):
-            if t == PACK - 1:
+            if t == last:
                 gather_gate(t, tag="h_bf11")
             scatter(t, HALF if t == 0 else 0, J)
             nc.sync.dma_start(out_rows[:, t, :], page[t][:])
             for u, (c0, c1) in enumerate(pieces):
                 src = page[t][:, c0:c1]
-                if t == PACK - 1 and u < VECTOR_PIECES:
+                if t == last and u < VECTOR_PIECES:
                     nc.vector.tensor_copy(out_bf[u][:, :, t], src)
-                elif t == PACK - 2 and u < VECTOR_PIECES:
+                elif t == last - 1 and u < VECTOR_PIECES:
                     nc.scalar.copy(out_bf[u][:, :, t : t + 2], src.unsqueeze(2).to_broadcast([P, c1 - c0, 2]))
                 else:
                     nc.scalar.copy(out_bf[u][:, :, t], src)
@@ -263,8 +275,9 @@ def tile_list_modp_gsilu_gateP_kernel(
                 in_=out_bf[u][:].rearrange("p c t -> p (c t)"),
             )
             nc.sync.dma_start(out_words[:, c0:c1], codes[:])
-        for q in range(4):
-            queue = nc.scalar if q % 2 else nc.sync
+        for quad in range(P // QUAD):
+            queue = nc.scalar if quad % 2 else nc.sync
             queue.dma_start(
-                out_2[0, 4 * q : 4 * q + 4, :].bitcast(I32), out_scale[QUAD * q : QUAD * q + 4, :].bitcast(I32)
+                out_2[0, 4 * quad : 4 * quad + 4, :].bitcast(I32),
+                out_scale[QUAD * quad : QUAD * quad + 4, :].bitcast(I32),
             )

@@ -27,11 +27,15 @@ GROUP = 16
 EDGES = (0, 512, 768, 1280, 1792, 2048)
 VECTOR_PIECES = 2
 
-AT_WG10, AT_TAB_SCALES, AT_WU = 0, 7, 8
-AT_TAB_WORDS, AT_WGO, AT_GATE0 = 12, 12, 16
-AT_PICKED, AT_WG01 = 24, 24
+AT_WG10, AT_WEIGHT_SCALES, AT_WU = 0, 7.5, 8
+AT_WGO, AT_TAB_SCALES, AT_GATE0 = 12, 15, 16
+AT_TAB_WORDS, AT_WG01 = 24, 24
 AT_WG00, AT_WG11 = 32, 32
 AT_GATE1, AT_GATE2, AT_GATE3 = AT_WG10, AT_WG01, AT_WG11
+AT_PICKED = 40
+ACT_AT = {(0, 1, 0): AT_WG01, (0, 1, 2): AT_WG11}
+AT_GATED0, AT_GATED1 = 44, 52
+AT_PAGE = (60, AT_GATE3, AT_GATED0, AT_GATED1)
 
 
 def tile_list_modp_gsilu_gateP_kernel(
@@ -48,19 +52,21 @@ def tile_list_modp_gsilu_gateP_kernel(
             return keep.tile(shape, dtype, name=name, tag=tag or name, align_bytes=64)
 
         def staged(name, shape, dtype, kib):
-            return shared.tile(shape, dtype, name=name, offset=1024 * kib)
+            return shared.tile(shape, dtype, name=name, offset=int(1024 * kib))
 
         offsets = keep.tile([P, J // GROUP], U16, name="offsets")
         nc.sync.dma_start(offsets[:], offs)
 
         ts_raw = staged("ts_raw", [P, T], U8, AT_TAB_SCALES)
-        ws_raw = sb("ws_raw", [P, R], U8)
-        nc.sync.dma_start(ts_raw[96:128, :].bitcast(I32), tab_scales.rearrange("a q t -> q a t").bitcast(I32))
+        ws_raw = staged("ws_raw", [P, R], U8, AT_WEIGHT_SCALES)
         nc.sync.dma_start(ws_raw[96:128, :].bitcast(I32), wu_scales.rearrange("a q r -> q a r").bitcast(I32))
         nc.sync.dma_start(ws_raw[64:96, 0:N].bitcast(I32), wd_scales.rearrange("a q n -> q a n").bitcast(I32))
+        nc.sync.dma_start(ts_raw[96:128, :].bitcast(I32), tab_scales.rearrange("a q t -> q a t").bitcast(I32))
         nc.vector.memset(ws_raw[0:64, :].bitcast(I32), 0)
         nc.vector.memset(ws_raw[64:96, N:R].bitcast(I32), 0)
         nc.vector.memset(ts_raw[0:96, :].bitcast(I32), 0)
+        page = {0: staged("page0", [P, T], F32, AT_PAGE[0])}
+        nc.vector.memset(page[0][:].bitcast(I32), 0)
 
         def place_scale_rows(queue, scale, rows):
             for quad in range(P // QUAD):
@@ -99,25 +105,25 @@ def tile_list_modp_gsilu_gateP_kernel(
             ws_raw[:].rearrange("p (b m t) -> p b t m", b=R // PASS, t=PACK),
         )
         wu_scale = sb("wu_scale", [P, PASSES, R], U8)
-        place_scale_rows(nc.scalar, wu_scale, ws_dealt[96:128, :])
+        place_scale_rows(nc.sync, wu_scale, ws_dealt[96:128, :])
+        load_wg(1, 0, AT_WG10)
+        load_wu(0)
 
         ts_picked = sb("ts_picked", [P, J], U8)
         nc.vector.tensor_copy(ts_picked[:], ts_raw[:].indirect(offsets[:]))
         tab_scale = sb("tab_scale", [P, PASSES, J], U8)
-        place_scale_rows(nc.scalar, tab_scale, ts_picked[96:128, :])
-        load_wg(1, 0, AT_WG10)
-        load_wu(0)
-
-        tab_picked = staged("tab_picked", [P, J], I32, AT_PICKED)
-        nc.vector.tensor_copy(tab_picked[:].bitcast(U32), tab_raw[:].bitcast(U32).indirect(offsets[:]))
+        place_scale_rows(nc.sync, tab_scale, ts_picked[96:128, :])
         wgo_sb = staged("wgo_sb", [P, J], F32, AT_WGO)
         nc.sync.dma_start(wgo_sb[:], wgo)
         load_gate(0, AT_GATE0)
+
+        tab_picked = staged("tab_picked", [P, J], I32, AT_PICKED)
+        nc.vector.tensor_copy(tab_picked[:].bitcast(U32), tab_raw[:].bitcast(U32).indirect(offsets[:]))
+        load_wg(0, 1, AT_WG01)
         tab_codes = sb("tab_codes", [P, PASSES, 2 * J], U8)
         nc.vector.tensor_copy(
             tab_codes[:].bitcast(U16), tab_picked[:].bitcast(U16).rearrange("p (j a) -> p a j", a=PASSES)
         )
-        load_wg(0, 1, AT_WG01)
 
         wu_codes = {}
 
@@ -142,8 +148,8 @@ def tile_list_modp_gsilu_gateP_kernel(
 
         gate = {}
 
-        def gather_gate(t, tag=None):
-            gate[t] = sb(f"gate{t}", [P, J], F32, tag=tag)
+        def gather_gate(t, tag=None, kib=None):
+            gate[t] = sb(f"gate{t}", [P, J], F32, tag=tag) if kib is None else staged(f"gate{t}", [P, J], F32, kib)
             nc.vector.tensor_tensor(gate[t][:], gate_raw[t][:].indirect(offsets[:]), wgo_sb[:], MULT)
 
         h_codes, h_scale = {}, {}
@@ -176,7 +182,10 @@ def tile_list_modp_gsilu_gateP_kernel(
                             start=(a == 0),
                             stop=(a == PASSES - 1),
                         )
-                act = ring.tile([P, P // 2, PACK, 2], F32, name="act")
+                if (b, half, s) in ACT_AT:
+                    act = staged(f"act{s}", [P, P // 2, PACK, 2], F32, ACT_AT[b, half, s])
+                else:
+                    act = ring.tile([P, P // 2, PACK, 2], F32, name="act")
                 nc.scalar.activation(act[:], ga[:].rearrange("p (t c e) -> p c t e", t=PACK, e=2), SILU)
                 nc.vector.tensor_tensor(
                     rounded[:, PACK * P * s : PACK * P * (s + 1)].rearrange("p (c e t) -> p c t e", t=PACK, e=2),
@@ -204,17 +213,15 @@ def tile_list_modp_gsilu_gateP_kernel(
                 )
             nc.scalar.copy(y_sb[t][:, HALF * half : HALF * (half + 1)], y[:])
 
-        page = [sb(f"page{t}", [P, T], F32) for t in range(PACK)]
-
         def scatter(t, j0, j1):
             nc.vector.tensor_tensor(
                 page[t][:].indirect(offsets[:, j0 // GROUP : j1 // GROUP]), y_sb[t][:, j0:j1], gate[t][:, j0:j1], MULT
             )
 
-        deal_wu(0)
-        load_wu(1)
         quantise_wg(0, 0)
         load_wg(1, 1, AT_WG11)
+        deal_wu(0)
+        load_wu(1)
         wd_scale = sb("wd_scale", [P, PASSES, N], U8, tag="wg_bf00")
         place_scale_rows(nc.sync, wd_scale, ws_dealt[64:96, 0:N])
         quantise_wg(1, 0)
@@ -222,29 +229,27 @@ def tile_list_modp_gsilu_gateP_kernel(
         wd_raw = sb("wd_raw", [P, PASSES, 2 * N], U8, tag="wg_bf10")
         nc.sync.dma_start(wd_raw[:].bitcast(I32), wd_words.rearrange("a p n -> p a n").bitcast(I32))
         hidden(0, 0)
-        gather_gate(0)
-        hidden(0, 1)
         quantise_wg(0, 1)
-        load_gate(2, AT_GATE2)
         quantise_wg(1, 1)
-        load_gate(3, AT_GATE3)
         deal_wu(1)
+        hidden(0, 1)
+        load_gate(2, AT_GATE2)
+        load_gate(3, AT_GATE3)
+        gather_gate(0, kib=AT_GATED0)
         wd_codes = sb("wd_codes", [P, PASSES, 2 * N], U8)
         nc.vector.tensor_copy(
             wd_codes[:].bitcast(U16).rearrange("p a (t m) -> p a m t", t=PACK),
             wd_raw[:].bitcast(U16).rearrange("p a (m t) -> p a m t", t=PACK),
         )
-        gather_gate(1)
+        gather_gate(1, kib=AT_GATED1)
         hidden(1, 0)
+        gather_gate(2)
         for t in range(PACK):
-            nc.vector.memset(page[t][:].bitcast(I32), 0)
-        down(0, 0)
+            down(t, 0)
         scatter(0, 0, HALF)
         hidden(1, 1)
-        gather_gate(2, tag="h_bf11")
-        down(0, 1)
-        for t in range(1, PACK):
-            down(t, 0)
+        gather_gate(3, tag="h_bf11")
+        for t in range(PACK):
             down(t, 1)
 
         pieces = list(zip(EDGES[:-1], EDGES[1:]))
@@ -252,8 +257,9 @@ def tile_list_modp_gsilu_gateP_kernel(
         out_rows = out_0.rearrange("(p t) c -> p t c", t=PACK)
         last = PACK - 1
         for t in range(PACK):
-            if t == last:
-                gather_gate(t, tag="h_bf11")
+            if t > 0:
+                page[t] = staged(f"page{t}", [P, T], F32, AT_PAGE[t])
+                nc.gpsimd.memset(page[t][:].bitcast(I32), 0)
             scatter(t, HALF if t == 0 else 0, J)
             nc.sync.dma_start(out_rows[:, t, :], page[t][:])
             for u, (c0, c1) in enumerate(pieces):

@@ -24,7 +24,7 @@ QUAD = 32
 HALF = J // 2
 GROUP = 16
 
-EDGES = (0, 512, 768, 1280, 1792, 2048)
+EDGES = (0, 512, 1024, 1536, 1792, 2048)
 VECTOR_PIECES = 2
 
 AT_WG10, AT_WEIGHT_SCALES, AT_WU = 0, 7.5, 8
@@ -34,8 +34,9 @@ AT_WG00, AT_WG11 = 32, 32
 AT_GATE1, AT_GATE2, AT_GATE3 = AT_WG10, AT_WG01, AT_WG11
 AT_PICKED = 40
 ACT_AT = {(0, 1, 0): AT_WG01, (0, 1, 2): AT_WG11}
-AT_GATED0, AT_GATED1 = 44, 52
-AT_PAGE = (60, AT_GATE3, AT_GATED0, AT_GATED1)
+AT_GATED0 = 44
+AT_PAGE = (52, AT_GATE3, AT_GATED0)
+PLANE = (2, 0, 1, 3)
 
 
 def tile_list_modp_gsilu_gateP_kernel(
@@ -69,7 +70,7 @@ def tile_list_modp_gsilu_gateP_kernel(
         nc.vector.memset(page[0][:].bitcast(I32), 0)
 
         def place_scale_rows(queue, scale, rows):
-            for quad in range(P // QUAD):
+            for quad in (0, 2, 1, 3):
                 queue.dma_start(
                     scale[QUAD * quad : QUAD * quad + 4].bitcast(I32), rows[8 * quad : 8 * (quad + 1)].bitcast(I32)
                 )
@@ -95,7 +96,7 @@ def tile_list_modp_gsilu_gateP_kernel(
 
         def load_gate(t, kib):
             gate_raw[t] = staged(f"gate_raw{t}", [P, T], F32, kib)
-            nc.sync.dma_start(gate_raw[t][:], gT.rearrange("(p t) c -> p t c", t=PACK)[:, t, :])
+            nc.sync.dma_start(gate_raw[t][:], gT.rearrange("(p t) c -> p t c", t=PACK)[:, PLANE[t], :])
 
         load_wg(0, 0, AT_WG00)
 
@@ -199,13 +200,14 @@ def tile_list_modp_gsilu_gateP_kernel(
 
         y_sb = [sb(f"y_sb{t}", [P, J], F32) for t in range(PACK)]
 
-        def down(t, half):
-            y = psum.tile([P, HALF], F32, name="y", tag="y", bufs=2)
+        def down(t, half, bank="y", bufs=2):
+            y = psum.tile([P, HALF], F32, name="y", tag=bank, bufs=bufs)
+            n0 = P * PLANE[t]
             for a in range(PASSES):
                 nc.tensor.matmul_mx(
                     out=y[:],
-                    lhsT=wd_codes[:, a, 2 * P * t : 2 * P * (t + 1)].bitcast(FP4X4),
-                    lhsT_scale=wd_scale[:, a, P * t : P * (t + 1)],
+                    lhsT=wd_codes[:, a, 2 * n0 : 2 * (n0 + P)].bitcast(FP4X4),
+                    lhsT_scale=wd_scale[:, a, n0 : n0 + P],
                     rhs=h_codes[a, half][:].bitcast(FP8X4),
                     rhs_scale=h_scale[a, half][:],
                     start=(a == 0),
@@ -241,7 +243,7 @@ def tile_list_modp_gsilu_gateP_kernel(
             wd_codes[:].bitcast(U16).rearrange("p a (t m) -> p a m t", t=PACK),
             wd_raw[:].bitcast(U16).rearrange("p a (m t) -> p a m t", t=PACK),
         )
-        gather_gate(1, kib=AT_GATED1)
+        gather_gate(1)
         hidden(1, 0)
         gather_gate(2)
         for t in range(PACK):
@@ -250,26 +252,27 @@ def tile_list_modp_gsilu_gateP_kernel(
         hidden(1, 1)
         gather_gate(3, tag="h_bf11")
         for t in range(PACK):
-            down(t, 1)
+            down(t, 1, ("ga", "ub")[t % 2], 3)
 
         pieces = list(zip(EDGES[:-1], EDGES[1:]))
-        out_bf = [sb(f"out_bf{c0}", [P, c1 - c0, PACK], BF16) for c0, c1 in pieces]
+        out_bf = sb("out_bf", [P, T, PACK], BF16, tag="h_codes11")
         out_rows = out_0.rearrange("(p t) c -> p t c", t=PACK)
         last = PACK - 1
         for t in range(PACK):
-            if t > 0:
+            if t == last:
+                page[t] = page[0]
+            elif t > 0:
                 page[t] = staged(f"page{t}", [P, T], F32, AT_PAGE[t])
                 nc.gpsimd.memset(page[t][:].bitcast(I32), 0)
             scatter(t, HALF if t == 0 else 0, J)
-            nc.sync.dma_start(out_rows[:, t, :], page[t][:])
-            for u, (c0, c1) in enumerate(pieces):
-                src = page[t][:, c0:c1]
-                if t == last and u < VECTOR_PIECES:
-                    nc.vector.tensor_copy(out_bf[u][:, :, t], src)
-                elif t == last - 1 and u < VECTOR_PIECES:
-                    nc.scalar.copy(out_bf[u][:, :, t : t + 2], src.unsqueeze(2).to_broadcast([P, c1 - c0, 2]))
-                else:
-                    nc.scalar.copy(out_bf[u][:, :, t], src)
+            queue = nc.scalar if t == last else nc.sync
+            queue.dma_start(out_rows[:, PLANE[t], :], page[t][:])
+            if t < last:
+                nc.scalar.copy(out_bf[:, :, PLANE[t]], page[t][:])
+            else:
+                for u, (c0, c1) in enumerate(pieces):
+                    copy = nc.vector.tensor_copy if u < VECTOR_PIECES else nc.scalar.copy
+                    copy(out_bf[:, c0:c1, PLANE[t]], page[t][:, c0:c1])
 
         out_scale = sb("out_scale", [P, T], U8)
         out_words = out_1[0].rearrange("p t i -> p (t i)").bitcast(I32)
@@ -278,11 +281,11 @@ def tile_list_modp_gsilu_gateP_kernel(
             nc.vector.quantize_mx(
                 out=codes[:].bitcast(FP8X4),
                 scales=out_scale[:, c0:c1],
-                in_=out_bf[u][:].rearrange("p c t -> p (c t)"),
+                in_=out_bf[:, c0:c1, :].rearrange("p c t -> p (c t)"),
             )
             nc.sync.dma_start(out_words[:, c0:c1], codes[:])
         for quad in range(P // QUAD):
-            queue = nc.scalar if quad % 2 else nc.sync
+            queue = nc.scalar if quad // 2 else nc.sync
             queue.dma_start(
                 out_2[0, 4 * quad : 4 * quad + 4, :].bitcast(I32),
                 out_scale[QUAD * quad : QUAD * quad + 4, :].bitcast(I32),

@@ -24,6 +24,8 @@ QUAD = 32
 HALF = J // 2
 GROUP = 16
 
+PLANE = (2, 0, 1, 3)
+
 EDGES = (0, 512, 1024, 1536, 1792, 2048)
 VECTOR_PIECES = 2
 
@@ -32,11 +34,9 @@ AT_WGO, AT_TAB_SCALES, AT_GATE0 = 12, 15, 16
 AT_TAB_WORDS, AT_WG01 = 24, 24
 AT_WG00, AT_WG11 = 32, 32
 AT_GATE1, AT_GATE2, AT_GATE3 = AT_WG10, AT_WG01, AT_WG11
-AT_PICKED = 40
+AT_PICKED, AT_GATED0 = 40, 44
 ACT_AT = {(0, 1, 0): AT_WG01, (0, 1, 2): AT_WG11}
-AT_GATED0 = 44
 AT_PAGE = (52, AT_GATE3, AT_GATED0)
-PLANE = (2, 0, 1, 3)
 
 
 def tile_list_modp_gsilu_gateP_kernel(
@@ -53,7 +53,7 @@ def tile_list_modp_gsilu_gateP_kernel(
             return keep.tile(shape, dtype, name=name, tag=tag or name, align_bytes=64)
 
         def staged(name, shape, dtype, kib):
-            return shared.tile(shape, dtype, name=name, offset=int(1024 * kib))
+            return shared.tile(shape, dtype, name=name, offset=int(1024 * kib), align_bytes=64)
 
         offsets = keep.tile([P, J // GROUP], U16, name="offsets")
         nc.sync.dma_start(offsets[:], offs)
@@ -69,9 +69,9 @@ def tile_list_modp_gsilu_gateP_kernel(
         page = {0: staged("page0", [P, T], F32, AT_PAGE[0])}
         nc.vector.memset(page[0][:].bitcast(I32), 0)
 
-        def place_scale_rows(queue, scale, rows):
+        def place_scale_rows(scale, rows):
             for quad in (0, 2, 1, 3):
-                queue.dma_start(
+                nc.sync.dma_start(
                     scale[QUAD * quad : QUAD * quad + 4].bitcast(I32), rows[8 * quad : 8 * (quad + 1)].bitcast(I32)
                 )
 
@@ -94,9 +94,9 @@ def tile_list_modp_gsilu_gateP_kernel(
 
         gate_raw = {}
 
-        def load_gate(t, kib):
-            gate_raw[t] = staged(f"gate_raw{t}", [P, T], F32, kib)
-            nc.sync.dma_start(gate_raw[t][:], gT.rearrange("(p t) c -> p t c", t=PACK)[:, PLANE[t], :])
+        def load_gate(u, kib):
+            gate_raw[u] = staged(f"gate_raw{u}", [P, T], F32, kib)
+            nc.sync.dma_start(gate_raw[u][:], gT.rearrange("(p t) c -> p t c", t=PACK)[:, PLANE[u], :])
 
         load_wg(0, 0, AT_WG00)
 
@@ -106,14 +106,14 @@ def tile_list_modp_gsilu_gateP_kernel(
             ws_raw[:].rearrange("p (b m t) -> p b t m", b=R // PASS, t=PACK),
         )
         wu_scale = sb("wu_scale", [P, PASSES, R], U8)
-        place_scale_rows(nc.sync, wu_scale, ws_dealt[96:128, :])
+        place_scale_rows(wu_scale, ws_dealt[96:128, :])
         load_wg(1, 0, AT_WG10)
         load_wu(0)
 
         ts_picked = sb("ts_picked", [P, J], U8)
         nc.vector.tensor_copy(ts_picked[:], ts_raw[:].indirect(offsets[:]))
         tab_scale = sb("tab_scale", [P, PASSES, J], U8)
-        place_scale_rows(nc.sync, tab_scale, ts_picked[96:128, :])
+        place_scale_rows(tab_scale, ts_picked[96:128, :])
         wgo_sb = staged("wgo_sb", [P, J], F32, AT_WGO)
         nc.sync.dma_start(wgo_sb[:], wgo)
         load_gate(0, AT_GATE0)
@@ -141,22 +141,26 @@ def tile_list_modp_gsilu_gateP_kernel(
             rounded = sb(f"wg_bf{a}{b}", [P, PACK * PASS], BF16)
             dst = rounded[:].rearrange("p (t m i) -> p m i t", t=PACK, i=PACK)
             src = wg_raw[a, b][:].rearrange("p i (m t) -> p m i t", t=PACK)
-            for m0 in range(0, P, P // 2):
-                nc.scalar.copy(dst[:, m0 : m0 + P // 2], src[:, m0 : m0 + P // 2])
+            nc.scalar.copy(dst[:, 0 : P // 2], src[:, 0 : P // 2])
+            copy = nc.vector.tensor_copy if (a, b) == (1, 1) else nc.scalar.copy
+            copy(dst[:, P // 2 : P], src[:, P // 2 : P])
             wg_codes[a, b] = sb(f"wg_codes{a}{b}", [P, PASS], U32)
             wg_scale[a, b] = sb(f"wg_scale{a}{b}", [P, PASS], U8)
             nc.vector.quantize_mx(out=wg_codes[a, b][:].bitcast(FP8X4), scales=wg_scale[a, b][:], in_=rounded[:])
 
         gate = {}
 
-        def gather_gate(t, tag=None, kib=None):
-            gate[t] = sb(f"gate{t}", [P, J], F32, tag=tag) if kib is None else staged(f"gate{t}", [P, J], F32, kib)
-            nc.vector.tensor_tensor(gate[t][:], gate_raw[t][:].indirect(offsets[:]), wgo_sb[:], MULT)
+        def gather_gate(u, tag=None, kib=None):
+            gate[u] = sb(f"gate{u}", [P, J], F32, tag=tag) if kib is None else staged(f"gate{u}", [P, J], F32, kib)
+            nc.vector.tensor_tensor(gate[u][:], gate_raw[u][:].indirect(offsets[:]), wgo_sb[:], MULT)
 
         h_codes, h_scale = {}, {}
 
         def hidden(b, half):
-            rounded = sb(f"h_bf{b}{half}", [P, PACK * HALF], BF16)
+            if (b, half) == (0, 0):
+                rounded = staged(f"h_bf{b}{half}", [P, PACK * HALF], BF16, AT_GATE0)
+            else:
+                rounded = sb(f"h_bf{b}{half}", [P, PACK * HALF], BF16)
             for s in range(HALF // P):
                 j0 = HALF * half + P * s
                 ga = psum.tile([P, PACK * P], F32, name="ga", tag="ga", bufs=3)
@@ -198,11 +202,11 @@ def tile_list_modp_gsilu_gateP_kernel(
             h_scale[b, half] = sb(f"h_scale{b}{half}", [P, HALF], U8)
             nc.vector.quantize_mx(out=h_codes[b, half][:].bitcast(FP8X4), scales=h_scale[b, half][:], in_=rounded[:])
 
-        y_sb = [sb(f"y_sb{t}", [P, J], F32) for t in range(PACK)]
+        y_sb = [sb(f"y_sb{u}", [P, J], F32) for u in range(PACK)]
 
-        def down(t, half, bank="y", bufs=2):
+        def down(u, half, bank="y", bufs=2):
             y = psum.tile([P, HALF], F32, name="y", tag=bank, bufs=bufs)
-            n0 = P * PLANE[t]
+            n0 = P * PLANE[u]
             for a in range(PASSES):
                 nc.tensor.matmul_mx(
                     out=y[:],
@@ -213,11 +217,11 @@ def tile_list_modp_gsilu_gateP_kernel(
                     start=(a == 0),
                     stop=(a == PASSES - 1),
                 )
-            nc.scalar.copy(y_sb[t][:, HALF * half : HALF * (half + 1)], y[:])
+            nc.scalar.copy(y_sb[u][:, HALF * half : HALF * (half + 1)], y[:])
 
-        def scatter(t, j0, j1):
+        def scatter(u, j0, j1):
             nc.vector.tensor_tensor(
-                page[t][:].indirect(offsets[:, j0 // GROUP : j1 // GROUP]), y_sb[t][:, j0:j1], gate[t][:, j0:j1], MULT
+                page[u][:].indirect(offsets[:, j0 // GROUP : j1 // GROUP]), y_sb[u][:, j0:j1], gate[u][:, j0:j1], MULT
             )
 
         quantise_wg(0, 0)
@@ -225,11 +229,12 @@ def tile_list_modp_gsilu_gateP_kernel(
         deal_wu(0)
         load_wu(1)
         wd_scale = sb("wd_scale", [P, PASSES, N], U8, tag="wg_bf00")
-        place_scale_rows(nc.sync, wd_scale, ws_dealt[64:96, 0:N])
+        place_scale_rows(wd_scale, ws_dealt[64:96, 0:N])
         quantise_wg(1, 0)
         load_gate(1, AT_GATE1)
         wd_raw = sb("wd_raw", [P, PASSES, 2 * N], U8, tag="wg_bf10")
         nc.sync.dma_start(wd_raw[:].bitcast(I32), wd_words.rearrange("a p n -> p a n").bitcast(I32))
+        gather_gate(0, kib=AT_GATED0)
         hidden(0, 0)
         quantise_wg(0, 1)
         quantise_wg(1, 1)
@@ -237,7 +242,6 @@ def tile_list_modp_gsilu_gateP_kernel(
         hidden(0, 1)
         load_gate(2, AT_GATE2)
         load_gate(3, AT_GATE3)
-        gather_gate(0, kib=AT_GATED0)
         wd_codes = sb("wd_codes", [P, PASSES, 2 * N], U8)
         nc.vector.tensor_copy(
             wd_codes[:].bitcast(U16).rearrange("p a (t m) -> p a m t", t=PACK),
@@ -246,38 +250,38 @@ def tile_list_modp_gsilu_gateP_kernel(
         gather_gate(1)
         hidden(1, 0)
         gather_gate(2)
-        for t in range(PACK):
-            down(t, 0)
+        for u in range(PACK):
+            down(u, 0)
         scatter(0, 0, HALF)
         hidden(1, 1)
         gather_gate(3, tag="h_bf11")
-        for t in range(PACK):
-            down(t, 1, ("ga", "ub")[t % 2], 3)
+        for u in range(PACK):
+            down(u, 1, ("ga", "ub")[u % 2], 3)
 
         pieces = list(zip(EDGES[:-1], EDGES[1:]))
         out_bf = sb("out_bf", [P, T, PACK], BF16, tag="h_codes11")
         out_rows = out_0.rearrange("(p t) c -> p t c", t=PACK)
         last = PACK - 1
-        for t in range(PACK):
-            if t == last:
-                page[t] = page[0]
-            elif t > 0:
-                page[t] = staged(f"page{t}", [P, T], F32, AT_PAGE[t])
-                nc.gpsimd.memset(page[t][:].bitcast(I32), 0)
-            scatter(t, HALF if t == 0 else 0, J)
-            queue = nc.scalar if t == last else nc.sync
-            queue.dma_start(out_rows[:, PLANE[t], :], page[t][:])
-            if t < last:
-                nc.scalar.copy(out_bf[:, :, PLANE[t]], page[t][:])
+        for u in range(PACK):
+            if u == last:
+                page[u] = page[0]
+            elif u > 0:
+                page[u] = staged(f"page{u}", [P, T], F32, AT_PAGE[u])
+                nc.gpsimd.memset(page[u][:].bitcast(I32), 0)
+            scatter(u, HALF if u == 0 else 0, J)
+            queue = nc.scalar if u == last else nc.sync
+            queue.dma_start(out_rows[:, PLANE[u], :], page[u][:])
+            if u < last:
+                nc.scalar.copy(out_bf[:, :, PLANE[u]], page[u][:])
             else:
-                for u, (c0, c1) in enumerate(pieces):
-                    copy = nc.vector.tensor_copy if u < VECTOR_PIECES else nc.scalar.copy
-                    copy(out_bf[:, c0:c1, PLANE[t]], page[t][:, c0:c1])
+                for piece, (c0, c1) in enumerate(pieces):
+                    copy = nc.vector.tensor_copy if piece < VECTOR_PIECES else nc.scalar.copy
+                    copy(out_bf[:, c0:c1, PLANE[u]], page[u][:, c0:c1])
 
         out_scale = sb("out_scale", [P, T], U8)
         out_words = out_1[0].rearrange("p t i -> p (t i)").bitcast(I32)
-        for u, (c0, c1) in enumerate(pieces):
-            codes = sb(f"out_codes{u}", [P, c1 - c0], I32)
+        for piece, (c0, c1) in enumerate(pieces):
+            codes = sb(f"out_codes{piece}", [P, c1 - c0], I32)
             nc.vector.quantize_mx(
                 out=codes[:].bitcast(FP8X4),
                 scales=out_scale[:, c0:c1],

@@ -115,8 +115,9 @@ def tile_list_modp_gsilu_gateP_kernel(
         tab_scale = sb("tab_scale", [P, PASSES, J], U8)
         place_scale_rows(tab_scale, ts_picked[96:128, :])
         wgo_sb = staged("wgo_sb", [P, J], F32, AT_WGO)
-        nc.sync.dma_start(wgo_sb[:], wgo)
+        nc.sync.dma_start(wgo_sb[:, 0:HALF], wgo[:, 0:HALF])
         load_gate(0, AT_GATE0)
+        nc.sync.dma_start(wgo_sb[:, HALF:J], wgo[:, HALF:J])
 
         tab_picked = staged("tab_picked", [P, J], I32, AT_PICKED)
         nc.vector.tensor_copy(tab_picked[:].bitcast(U32), tab_raw[:].bitcast(U32).indirect(offsets[:]))
@@ -152,7 +153,10 @@ def tile_list_modp_gsilu_gateP_kernel(
 
         def gather_gate(u, tag=None, kib=None):
             gate[u] = sb(f"gate{u}", [P, J], F32, tag=tag) if kib is None else staged(f"gate{u}", [P, J], F32, kib)
-            nc.vector.tensor_tensor(gate[u][:], gate_raw[u][:].indirect(offsets[:]), wgo_sb[:], MULT)
+            step = HALF if u == 0 else J
+            for j0 in range(0, J, step):
+                listed = gate_raw[u][:].indirect(offsets[:, j0 // GROUP : (j0 + step) // GROUP])
+                nc.vector.tensor_tensor(gate[u][:, j0 : j0 + step], listed, wgo_sb[:, j0 : j0 + step], MULT)
 
         h_codes, h_scale = {}, {}
 

@@ -1,6 +1,7 @@
 from contextlib import ExitStack
 
 import concourse.mybir as mybir
+from concourse.masks import make_identity
 
 K, R, N, T, J = 1024, 1024, 512, 2048, 1024
 FLOPS = 2 * J * (2 * K * R + R * N)
@@ -29,13 +30,13 @@ PLANE = (2, 0, 1, 3)
 EDGES = (0, 512, 1024, 1536, 1792, 2048)
 VECTOR_PIECES = 2
 
-AT_WG10, AT_WEIGHT_SCALES, AT_WU = 0, 7.5, 8
-AT_WGO, AT_TAB_SCALES, AT_GATE0 = 12, 15, 16
+AT_WEIGHT_SCALES, AT_GATE0 = 16, 16
+AT_TAB_SCALES, AT_WG10 = 59, 60
 AT_TAB_WORDS, AT_WG01 = 24, 24
 AT_WG00, AT_WG11 = 32, 32
 AT_GATE1, AT_GATE2, AT_GATE3 = AT_WG10, AT_WG01, AT_WG11
 AT_PICKED, AT_GATED0 = 40, 44
-ACT_AT = {(0, 1, 0): AT_WG01, (0, 1, 2): AT_WG11}
+ACT_AT = {(0, 0, 0): AT_GATED0, (0, 1, 0): AT_WG01, (0, 1, 2): AT_WG11}
 AT_PAGE = (52, AT_GATE3, AT_GATED0)
 
 
@@ -60,14 +61,31 @@ def tile_list_modp_gsilu_gateP_kernel(
 
         ts_raw = staged("ts_raw", [P, T], U8, AT_TAB_SCALES)
         ws_raw = staged("ws_raw", [P, R], U8, AT_WEIGHT_SCALES)
+        nc.sync.dma_start(ts_raw[96:128, :].bitcast(I32), tab_scales.rearrange("a q t -> q a t").bitcast(I32))
         nc.sync.dma_start(ws_raw[96:128, :].bitcast(I32), wu_scales.rearrange("a q r -> q a r").bitcast(I32))
         nc.sync.dma_start(ws_raw[64:96, 0:N].bitcast(I32), wd_scales.rearrange("a q n -> q a n").bitcast(I32))
-        nc.sync.dma_start(ts_raw[96:128, :].bitcast(I32), tab_scales.rearrange("a q t -> q a t").bitcast(I32))
+        cold = sb("cold", [P, 1], F32)
+        nc.vector.memset(cold[:], 0)
+        nc.vector.memset(ts_raw[0:96, :].bitcast(I32), 0)
         nc.vector.memset(ws_raw[0:64, :].bitcast(I32), 0)
         nc.vector.memset(ws_raw[64:96, N:R].bitcast(I32), 0)
-        nc.vector.memset(ts_raw[0:96, :].bitcast(I32), 0)
-        page = {0: staged("page0", [P, T], F32, AT_PAGE[0])}
-        nc.vector.memset(page[0][:].bitcast(I32), 0)
+
+        wgo_row = sb("wgo_row", [P, J // P], F32)
+        nc.sync.dma_start(wgo_row[:], wgo[0].rearrange("(p c) -> p c", p=P))
+        identity = sb("identity", [P, P], F32)
+        make_identity(nc, identity[:])
+        warm = sb("warm", [P, 1], F32)
+        nc.scalar.activation(warm[:], cold[:], SILU)
+        wgo_sb = sb("wgo_sb", [P, J], F32)
+        for g in range(J // HALF):
+            spread = psum.tile([P, HALF], F32, name="spread", tag="y", bufs=2)
+            for c in range(PACK):
+                column = wgo_row[:, PACK * g + c : PACK * g + c + 1]
+                nc.tensor.transpose(spread[:, P * c : P * (c + 1)], column.to_broadcast([P, P]), identity[:])
+            nc.scalar.copy(
+                wgo_sb[:].rearrange("p (k g c) -> p g k c", g=J // HALF, c=PACK)[:, g],
+                spread[:].rearrange("p (c k) -> p k c", c=PACK),
+            )
 
         def place_scale_rows(scale, rows):
             for quad in (0, 2, 1, 3):
@@ -87,8 +105,8 @@ def tile_list_modp_gsilu_gateP_kernel(
 
         wu_raw = {}
 
-        def load_wu(b):
-            wu_raw[b] = staged(f"wu_raw{b}", [P, PASSES, PASS], I32, AT_WU)
+        def load_wu(b, tag=None):
+            wu_raw[b] = sb(f"wu_raw{b}", [P, PASSES, PASS], I32, tag=tag)
             words = wu_words.rearrange("a p r i -> p a (r i)")
             nc.sync.dma_start(wu_raw[b][:], words[:, :, PACK * PASS * b : PACK * PASS * (b + 1)].bitcast(I32))
 
@@ -99,6 +117,15 @@ def tile_list_modp_gsilu_gateP_kernel(
             nc.sync.dma_start(gate_raw[u][:], gT.rearrange("(p t) c -> p t c", t=PACK)[:, PLANE[u], :])
 
         load_wg(0, 0, AT_WG00)
+        load_wu(0)
+
+        ts_picked = sb("ts_picked", [P, J], U8)
+        nc.vector.tensor_copy(ts_picked[:], ts_raw[:].indirect(offsets[:]))
+        tab_scale = sb("tab_scale", [P, PASSES, J], U8)
+        place_scale_rows(tab_scale, ts_picked[96:128, :])
+        load_wg(1, 0, AT_WG10)
+        page = {0: staged("page0", [P, T], F32, AT_PAGE[0])}
+        nc.gpsimd.memset(page[0][:].bitcast(I32), 0)
 
         ws_dealt = sb("ws_dealt", [P, R], U8)
         nc.vector.tensor_copy(
@@ -107,17 +134,7 @@ def tile_list_modp_gsilu_gateP_kernel(
         )
         wu_scale = sb("wu_scale", [P, PASSES, R], U8)
         place_scale_rows(wu_scale, ws_dealt[96:128, :])
-        load_wg(1, 0, AT_WG10)
-        load_wu(0)
-
-        ts_picked = sb("ts_picked", [P, J], U8)
-        nc.vector.tensor_copy(ts_picked[:], ts_raw[:].indirect(offsets[:]))
-        tab_scale = sb("tab_scale", [P, PASSES, J], U8)
-        place_scale_rows(tab_scale, ts_picked[96:128, :])
-        wgo_sb = staged("wgo_sb", [P, J], F32, AT_WGO)
-        nc.sync.dma_start(wgo_sb[:, 0:HALF], wgo[:, 0:HALF])
         load_gate(0, AT_GATE0)
-        nc.sync.dma_start(wgo_sb[:, HALF:J], wgo[:, HALF:J])
 
         tab_picked = staged("tab_picked", [P, J], I32, AT_PICKED)
         nc.vector.tensor_copy(tab_picked[:].bitcast(U32), tab_raw[:].bitcast(U32).indirect(offsets[:]))
@@ -143,7 +160,7 @@ def tile_list_modp_gsilu_gateP_kernel(
             dst = rounded[:].rearrange("p (t m i) -> p m i t", t=PACK, i=PACK)
             src = wg_raw[a, b][:].rearrange("p i (m t) -> p m i t", t=PACK)
             nc.scalar.copy(dst[:, 0 : P // 2], src[:, 0 : P // 2])
-            copy = nc.vector.tensor_copy if (a, b) == (1, 1) else nc.scalar.copy
+            copy = nc.vector.tensor_copy if a == 1 else nc.scalar.copy
             copy(dst[:, P // 2 : P], src[:, P // 2 : P])
             wg_codes[a, b] = sb(f"wg_codes{a}{b}", [P, PASS], U32)
             wg_scale[a, b] = sb(f"wg_scale{a}{b}", [P, PASS], U8)
@@ -153,32 +170,26 @@ def tile_list_modp_gsilu_gateP_kernel(
 
         def gather_gate(u, tag=None, kib=None):
             gate[u] = sb(f"gate{u}", [P, J], F32, tag=tag) if kib is None else staged(f"gate{u}", [P, J], F32, kib)
-            step = HALF if u == 0 else J
-            for j0 in range(0, J, step):
-                listed = gate_raw[u][:].indirect(offsets[:, j0 // GROUP : (j0 + step) // GROUP])
-                nc.vector.tensor_tensor(gate[u][:, j0 : j0 + step], listed, wgo_sb[:, j0 : j0 + step], MULT)
+            nc.vector.tensor_tensor(gate[u][:], gate_raw[u][:].indirect(offsets[:]), wgo_sb[:], MULT)
 
         h_codes, h_scale = {}, {}
 
         def hidden(b, half):
-            if (b, half) == (0, 0):
-                rounded = staged(f"h_bf{b}{half}", [P, PACK * HALF], BF16, AT_GATE0)
-            else:
-                rounded = sb(f"h_bf{b}{half}", [P, PACK * HALF], BF16)
+            rounded = sb(f"h_bf{b}{half}", [P, PACK * HALF], BF16)
             for s in range(HALF // P):
                 j0 = HALF * half + P * s
                 ga = psum.tile([P, PACK * P], F32, name="ga", tag="ga", bufs=3)
                 ub = psum.tile([P, PACK * P], F32, name="ub", tag="ub", bufs=3)
-                for t in range(PACK):
-                    for a in range(PASSES):
+                for a in range(PASSES):
+                    for t in range(PACK):
                         nc.tensor.matmul_mx(
                             out=ga[:, P * t : P * (t + 1)],
                             lhsT=wg_codes[a, b][:, P * t : P * (t + 1)].bitcast(FP8X4),
                             lhsT_scale=wg_scale[a, b][:, P * t : P * (t + 1)],
                             rhs=tab_codes[:, a, 2 * j0 : 2 * (j0 + P)].bitcast(FP4X4),
                             rhs_scale=tab_scale[:, a, j0 : j0 + P],
-                            start=(a == 0),
-                            stop=(a == PASSES - 1),
+                            start=(a, t) == (0, 0),
+                            stop=(a, t) == (PASSES - 1, PACK - 1),
                         )
                 for t in range(PACK):
                     for a in range(PASSES):
@@ -202,6 +213,8 @@ def tile_list_modp_gsilu_gateP_kernel(
                     act[:],
                     MULT,
                 )
+                if (b, half, s) == (0, 0, 0):
+                    gather_gate(0, kib=AT_GATED0)
             h_codes[b, half] = sb(f"h_codes{b}{half}", [P, HALF], U32)
             h_scale[b, half] = sb(f"h_scale{b}{half}", [P, HALF], U8)
             nc.vector.quantize_mx(out=h_codes[b, half][:].bitcast(FP8X4), scales=h_scale[b, half][:], in_=rounded[:])
@@ -231,18 +244,17 @@ def tile_list_modp_gsilu_gateP_kernel(
         quantise_wg(0, 0)
         load_wg(1, 1, AT_WG11)
         deal_wu(0)
-        load_wu(1)
-        wd_scale = sb("wd_scale", [P, PASSES, N], U8, tag="wg_bf00")
-        place_scale_rows(wd_scale, ws_dealt[64:96, 0:N])
         quantise_wg(1, 0)
+        load_wu(1, tag="wg_bf00")
         load_gate(1, AT_GATE1)
         wd_raw = sb("wd_raw", [P, PASSES, 2 * N], U8, tag="wg_bf10")
         nc.sync.dma_start(wd_raw[:].bitcast(I32), wd_words.rearrange("a p n -> p a n").bitcast(I32))
-        gather_gate(0, kib=AT_GATED0)
         hidden(0, 0)
         quantise_wg(0, 1)
         quantise_wg(1, 1)
         deal_wu(1)
+        wd_scale = sb("wd_scale", [P, PASSES, N], U8, tag="wg_bf00")
+        place_scale_rows(wd_scale, ws_dealt[64:96, 0:N])
         hidden(0, 1)
         load_gate(2, AT_GATE2)
         load_gate(3, AT_GATE3)

@@ -30,13 +30,15 @@ PLANE = (2, 0, 1, 3)
 EDGES = (0, 512, 1024, 1536, 1792, 2048)
 VECTOR_PIECES = 2
 
-AT_WEIGHT_SCALES, AT_GATE0 = 16, 16
-AT_TAB_SCALES, AT_WG10 = 59, 60
-AT_TAB_WORDS, AT_WG01 = 24, 24
-AT_WG00, AT_WG11 = 32, 32
+AT_WG10 = 68
+AT_WU0, AT_PICKED_SCALES, AT_WD = 4, 7.5, 8
+AT_TAB_SCALES = 58
+AT_WU1, AT_TAB_WORDS, AT_GATE0 = 12, 14, 20
+AT_WG01, AT_WG00 = 32, 32
+AT_ROUNDED00, AT_WG11 = 60, 60
 AT_GATE1, AT_GATE2, AT_GATE3 = AT_WG10, AT_WG01, AT_WG11
 AT_PICKED, AT_GATED0 = 40, 44
-ACT_AT = {(0, 0, 0): AT_GATED0, (0, 1, 0): AT_WG01, (0, 1, 2): AT_WG11}
+ACT_AT = {(0, 0, 2): AT_GATED0, (0, 1, 2): AT_WG01, (0, 1, 3): AT_WG11}
 AT_PAGE = (52, AT_GATE3, AT_GATED0)
 
 
@@ -60,7 +62,7 @@ def tile_list_modp_gsilu_gateP_kernel(
         nc.sync.dma_start(offsets[:], offs)
 
         ts_raw = staged("ts_raw", [P, T], U8, AT_TAB_SCALES)
-        ws_raw = staged("ws_raw", [P, R], U8, AT_WEIGHT_SCALES)
+        ws_raw = sb("ws_raw", [P, R], U8)
         nc.sync.dma_start(ts_raw[96:128, :].bitcast(I32), tab_scales.rearrange("a q t -> q a t").bitcast(I32))
         nc.sync.dma_start(ws_raw[96:128, :].bitcast(I32), wu_scales.rearrange("a q r -> q a r").bitcast(I32))
         nc.sync.dma_start(ws_raw[64:96, 0:N].bitcast(I32), wd_scales.rearrange("a q n -> q a n").bitcast(I32))
@@ -105,8 +107,8 @@ def tile_list_modp_gsilu_gateP_kernel(
 
         wu_raw = {}
 
-        def load_wu(b, tag=None):
-            wu_raw[b] = sb(f"wu_raw{b}", [P, PASSES, PASS], I32, tag=tag)
+        def load_wu(b):
+            wu_raw[b] = staged(f"wu_raw{b}", [P, PASSES, PASS], I32, (AT_WU0, AT_WU1)[b])
             words = wu_words.rearrange("a p r i -> p a (r i)")
             nc.sync.dma_start(wu_raw[b][:], words[:, :, PACK * PASS * b : PACK * PASS * (b + 1)].bitcast(I32))
 
@@ -117,32 +119,37 @@ def tile_list_modp_gsilu_gateP_kernel(
             nc.sync.dma_start(gate_raw[u][:], gT.rearrange("(p t) c -> p t c", t=PACK)[:, PLANE[u], :])
 
         load_wg(0, 0, AT_WG00)
-        load_wu(0)
-
-        ts_picked = sb("ts_picked", [P, J], U8)
-        nc.vector.tensor_copy(ts_picked[:], ts_raw[:].indirect(offsets[:]))
-        tab_scale = sb("tab_scale", [P, PASSES, J], U8)
-        place_scale_rows(tab_scale, ts_picked[96:128, :])
         load_wg(1, 0, AT_WG10)
+
+        ts_picked = staged("ts_picked", [P, J], U8, AT_PICKED_SCALES)
+        nc.vector.tensor_copy(ts_picked[:], ts_raw[:].indirect(offsets[:]))
         page = {0: staged("page0", [P, T], F32, AT_PAGE[0])}
         nc.gpsimd.memset(page[0][:].bitcast(I32), 0)
 
-        ws_dealt = sb("ws_dealt", [P, R], U8)
+        rows = sb("rows", [P, R + J], U8)
+        ws_dealt = rows[:, 0:R]
         nc.vector.tensor_copy(
-            ws_dealt[:].rearrange("p (b t m) -> p b t m", b=R // PASS, t=PACK),
+            ws_dealt.rearrange("p (b t m) -> p b t m", b=R // PASS, t=PACK),
             ws_raw[:].rearrange("p (b m t) -> p b t m", b=R // PASS, t=PACK),
         )
-        wu_scale = sb("wu_scale", [P, PASSES, R], U8)
-        place_scale_rows(wu_scale, ws_dealt[96:128, :])
-        load_gate(0, AT_GATE0)
+        nc.vector.tensor_copy(rows[96:128, R:].bitcast(I32), ts_picked[96:128, :].bitcast(I32))
+        placed = sb("placed", [P, PASSES, R + J], U8)
+        place_scale_rows(placed, rows[96:128, :])
+        wu_scale, tab_scale = placed[:, :, 0:R], placed[:, :, R:]
+        load_wu(0)
+        wd_raw = staged("wd_raw", [P, PASSES, 2 * N], U8, AT_WD)
+        nc.sync.dma_start(wd_raw[:].bitcast(I32), wd_words.rearrange("a p n -> p a n").bitcast(I32))
 
         tab_picked = staged("tab_picked", [P, J], I32, AT_PICKED)
-        nc.vector.tensor_copy(tab_picked[:].bitcast(U32), tab_raw[:].bitcast(U32).indirect(offsets[:]))
-        load_wg(0, 1, AT_WG01)
-        tab_codes = sb("tab_codes", [P, PASSES, 2 * J], U8)
-        nc.vector.tensor_copy(
-            tab_codes[:].bitcast(U16), tab_picked[:].bitcast(U16).rearrange("p (j a) -> p a j", a=PASSES)
-        )
+        for j0 in range(0, J, HALF):
+            listed = tab_raw[:].bitcast(U32).indirect(offsets[:, j0 // GROUP : (j0 + HALF) // GROUP])
+            nc.vector.tensor_copy(tab_picked[:, j0 : j0 + HALF].bitcast(U32), listed)
+        load_wu(1)
+        load_gate(0, AT_GATE0)
+        tab_codes = [sb(f"tab_codes{half}", [P, PASSES, 2 * HALF], U8) for half in range(J // HALF)]
+        for half in range(J // HALF):
+            words = tab_picked[:, HALF * half : HALF * (half + 1)].bitcast(U16)
+            nc.vector.tensor_copy(tab_codes[half][:].bitcast(U16), words.rearrange("p (j a) -> p a j", a=PASSES))
 
         wu_codes = {}
 
@@ -156,13 +163,19 @@ def tile_list_modp_gsilu_gateP_kernel(
         wg_codes, wg_scale = {}, {}
 
         def quantise_wg(a, b):
-            rounded = sb(f"wg_bf{a}{b}", [P, PACK * PASS], BF16)
+            if (a, b) == (0, 0):
+                rounded = staged("wg_bf00", [P, PACK * PASS], BF16, AT_ROUNDED00)
+            else:
+                rounded = sb(f"wg_bf{a}{b}", [P, PACK * PASS], BF16)
             dst = rounded[:].rearrange("p (t m i) -> p m i t", t=PACK, i=PACK)
             src = wg_raw[a, b][:].rearrange("p i (m t) -> p m i t", t=PACK)
             nc.scalar.copy(dst[:, 0 : P // 2], src[:, 0 : P // 2])
-            copy = nc.vector.tensor_copy if a == 1 else nc.scalar.copy
+            copy = nc.vector.tensor_copy if (a, b) == (1, 1) else nc.scalar.copy
             copy(dst[:, P // 2 : P], src[:, P // 2 : P])
-            wg_codes[a, b] = sb(f"wg_codes{a}{b}", [P, PASS], U32)
+            if (a, b) == (1, 0):
+                wg_codes[a, b] = staged("wg_codes10", [P, PASS], U32, AT_WU0)
+            else:
+                wg_codes[a, b] = sb(f"wg_codes{a}{b}", [P, PASS], U32)
             wg_scale[a, b] = sb(f"wg_scale{a}{b}", [P, PASS], U8)
             nc.vector.quantize_mx(out=wg_codes[a, b][:].bitcast(FP8X4), scales=wg_scale[a, b][:], in_=rounded[:])
 
@@ -186,7 +199,7 @@ def tile_list_modp_gsilu_gateP_kernel(
                             out=ga[:, P * t : P * (t + 1)],
                             lhsT=wg_codes[a, b][:, P * t : P * (t + 1)].bitcast(FP8X4),
                             lhsT_scale=wg_scale[a, b][:, P * t : P * (t + 1)],
-                            rhs=tab_codes[:, a, 2 * j0 : 2 * (j0 + P)].bitcast(FP4X4),
+                            rhs=tab_codes[half][:, a, 2 * P * s : 2 * P * (s + 1)].bitcast(FP4X4),
                             rhs_scale=tab_scale[:, a, j0 : j0 + P],
                             start=(a, t) == (0, 0),
                             stop=(a, t) == (PASSES - 1, PACK - 1),
@@ -197,7 +210,7 @@ def tile_list_modp_gsilu_gateP_kernel(
                             out=ub[:, P * t : P * (t + 1)],
                             lhsT=wu_codes[b][:, a, P * t : P * (t + 1)].bitcast(FP8X4),
                             lhsT_scale=wu_scale[:, a, PASS * b + P * t : PASS * b + P * (t + 1)],
-                            rhs=tab_codes[:, a, 2 * j0 : 2 * (j0 + P)].bitcast(FP4X4),
+                            rhs=tab_codes[half][:, a, 2 * P * s : 2 * P * (s + 1)].bitcast(FP4X4),
                             rhs_scale=tab_scale[:, a, j0 : j0 + P],
                             start=(a == 0),
                             stop=(a == PASSES - 1),
@@ -213,7 +226,7 @@ def tile_list_modp_gsilu_gateP_kernel(
                     act[:],
                     MULT,
                 )
-                if (b, half, s) == (0, 0, 0):
+                if (b, half, s) == (0, 0, 2):
                     gather_gate(0, kib=AT_GATED0)
             h_codes[b, half] = sb(f"h_codes{b}{half}", [P, HALF], U32)
             h_scale[b, half] = sb(f"h_scale{b}{half}", [P, HALF], U8)
@@ -242,27 +255,25 @@ def tile_list_modp_gsilu_gateP_kernel(
             )
 
         quantise_wg(0, 0)
+        load_wg(0, 1, AT_WG01)
         load_wg(1, 1, AT_WG11)
         deal_wu(0)
         quantise_wg(1, 0)
-        load_wu(1, tag="wg_bf00")
         load_gate(1, AT_GATE1)
-        wd_raw = sb("wd_raw", [P, PASSES, 2 * N], U8, tag="wg_bf10")
-        nc.sync.dma_start(wd_raw[:].bitcast(I32), wd_words.rearrange("a p n -> p a n").bitcast(I32))
-        hidden(0, 0)
-        quantise_wg(0, 1)
-        quantise_wg(1, 1)
-        deal_wu(1)
-        wd_scale = sb("wd_scale", [P, PASSES, N], U8, tag="wg_bf00")
-        place_scale_rows(wd_scale, ws_dealt[64:96, 0:N])
-        hidden(0, 1)
-        load_gate(2, AT_GATE2)
-        load_gate(3, AT_GATE3)
         wd_codes = sb("wd_codes", [P, PASSES, 2 * N], U8)
         nc.vector.tensor_copy(
             wd_codes[:].bitcast(U16).rearrange("p a (t m) -> p a m t", t=PACK),
             wd_raw[:].bitcast(U16).rearrange("p a (m t) -> p a m t", t=PACK),
         )
+        deal_wu(1)
+        hidden(0, 0)
+        quantise_wg(0, 1)
+        quantise_wg(1, 1)
+        wd_scale = sb("wd_scale", [P, PASSES, N], U8, tag="wg_bf01")
+        place_scale_rows(wd_scale, rows[64:96, 0:N])
+        hidden(0, 1)
+        load_gate(2, AT_GATE2)
+        load_gate(3, AT_GATE3)
         gather_gate(1)
         hidden(1, 0)
         gather_gate(2)

@@ -30,16 +30,16 @@ PLANE = (2, 0, 1, 3)
 EDGES = (0, 512, 1024, 1536, 1792, 2048)
 VECTOR_PIECES = 2
 
-AT_WG10 = 68
 AT_WU0, AT_PICKED_SCALES, AT_WD = 4, 7.5, 8
-AT_TAB_SCALES = 58
 AT_WU1, AT_TAB_WORDS, AT_GATE0 = 12, 14, 20
-AT_WG01, AT_WG00 = 32, 32
+AT_WG00, AT_WG01 = 32, 32
+AT_PICKED_WORDS, AT_GATED0 = 40, 44
+AT_PAGE0, AT_TAB_SCALES = 52, 58
 AT_ROUNDED00, AT_WG11 = 60, 60
+AT_WG10 = 68
 AT_GATE1, AT_GATE2, AT_GATE3 = AT_WG10, AT_WG01, AT_WG11
-AT_PICKED, AT_GATED0 = 40, 44
-ACT_AT = {(0, 0, 2): AT_GATED0, (0, 1, 2): AT_WG01, (0, 1, 3): AT_WG11}
-AT_PAGE = (52, AT_GATE3, AT_GATED0)
+ACT_AT = {(0, 1, 2): AT_WG01, (0, 1, 3): AT_WG11}
+AT_PAGE = (AT_PAGE0, AT_GATE3, AT_GATED0)
 
 
 def tile_list_modp_gsilu_gateP_kernel(
@@ -66,8 +66,8 @@ def tile_list_modp_gsilu_gateP_kernel(
         nc.sync.dma_start(ts_raw[96:128, :].bitcast(I32), tab_scales.rearrange("a q t -> q a t").bitcast(I32))
         nc.sync.dma_start(ws_raw[96:128, :].bitcast(I32), wu_scales.rearrange("a q r -> q a r").bitcast(I32))
         nc.sync.dma_start(ws_raw[64:96, 0:N].bitcast(I32), wd_scales.rearrange("a q n -> q a n").bitcast(I32))
-        cold = sb("cold", [P, 1], F32)
-        nc.vector.memset(cold[:], 0)
+        warm_in = sb("warm_in", [P, 1], F32)
+        nc.vector.memset(warm_in[:], 0)
         nc.vector.memset(ts_raw[0:96, :].bitcast(I32), 0)
         nc.vector.memset(ws_raw[0:64, :].bitcast(I32), 0)
         nc.vector.memset(ws_raw[64:96, N:R].bitcast(I32), 0)
@@ -76,8 +76,8 @@ def tile_list_modp_gsilu_gateP_kernel(
         nc.sync.dma_start(wgo_row[:], wgo[0].rearrange("(p c) -> p c", p=P))
         identity = sb("identity", [P, P], F32)
         make_identity(nc, identity[:])
-        warm = sb("warm", [P, 1], F32)
-        nc.scalar.activation(warm[:], cold[:], SILU)
+        warm_out = sb("warm_out", [P, 1], F32)
+        nc.scalar.activation(warm_out[:], warm_in[:], SILU)
         wgo_sb = sb("wgo_sb", [P, J], F32)
         for g in range(J // HALF):
             spread = psum.tile([P, HALF], F32, name="spread", tag="y", bufs=2)
@@ -126,26 +126,25 @@ def tile_list_modp_gsilu_gateP_kernel(
         page = {0: staged("page0", [P, T], F32, AT_PAGE[0])}
         nc.gpsimd.memset(page[0][:].bitcast(I32), 0)
 
-        rows = sb("rows", [P, R + J], U8)
-        ws_dealt = rows[:, 0:R]
+        scale_rows = sb("scale_rows", [P, R + J], U8)
         nc.vector.tensor_copy(
-            ws_dealt.rearrange("p (b t m) -> p b t m", b=R // PASS, t=PACK),
+            scale_rows[:, 0:R].rearrange("p (b t m) -> p b t m", b=R // PASS, t=PACK),
             ws_raw[:].rearrange("p (b m t) -> p b t m", b=R // PASS, t=PACK),
         )
-        nc.vector.tensor_copy(rows[96:128, R:].bitcast(I32), ts_picked[96:128, :].bitcast(I32))
+        nc.vector.tensor_copy(scale_rows[96:128, R:].bitcast(I32), ts_picked[96:128, :].bitcast(I32))
         placed = sb("placed", [P, PASSES, R + J], U8)
-        place_scale_rows(placed, rows[96:128, :])
+        place_scale_rows(placed, scale_rows[96:128, :])
         wu_scale, tab_scale = placed[:, :, 0:R], placed[:, :, R:]
         load_wu(0)
         wd_raw = staged("wd_raw", [P, PASSES, 2 * N], U8, AT_WD)
         nc.sync.dma_start(wd_raw[:].bitcast(I32), wd_words.rearrange("a p n -> p a n").bitcast(I32))
 
-        tab_picked = staged("tab_picked", [P, J], I32, AT_PICKED)
+        tab_picked = staged("tab_picked", [P, J], I32, AT_PICKED_WORDS)
         for j0 in range(0, J, HALF):
             listed = tab_raw[:].bitcast(U32).indirect(offsets[:, j0 // GROUP : (j0 + HALF) // GROUP])
             nc.vector.tensor_copy(tab_picked[:, j0 : j0 + HALF].bitcast(U32), listed)
-        load_wu(1)
         load_gate(0, AT_GATE0)
+        load_wu(1)
         tab_codes = [sb(f"tab_codes{half}", [P, PASSES, 2 * HALF], U8) for half in range(J // HALF)]
         for half in range(J // HALF):
             words = tab_picked[:, HALF * half : HALF * (half + 1)].bitcast(U16)
@@ -188,7 +187,10 @@ def tile_list_modp_gsilu_gateP_kernel(
         h_codes, h_scale = {}, {}
 
         def hidden(b, half):
-            rounded = sb(f"h_bf{b}{half}", [P, PACK * HALF], BF16)
+            if (b, half) == (0, 0):
+                rounded = staged("h_bf00", [P, PACK * HALF], BF16, AT_GATE0)
+            else:
+                rounded = sb(f"h_bf{b}{half}", [P, PACK * HALF], BF16)
             for s in range(HALF // P):
                 j0 = HALF * half + P * s
                 ga = psum.tile([P, PACK * P], F32, name="ga", tag="ga", bufs=3)
@@ -226,8 +228,6 @@ def tile_list_modp_gsilu_gateP_kernel(
                     act[:],
                     MULT,
                 )
-                if (b, half, s) == (0, 0, 2):
-                    gather_gate(0, kib=AT_GATED0)
             h_codes[b, half] = sb(f"h_codes{b}{half}", [P, HALF], U32)
             h_scale[b, half] = sb(f"h_scale{b}{half}", [P, HALF], U8)
             nc.vector.quantize_mx(out=h_codes[b, half][:].bitcast(FP8X4), scales=h_scale[b, half][:], in_=rounded[:])
@@ -265,12 +265,13 @@ def tile_list_modp_gsilu_gateP_kernel(
             wd_codes[:].bitcast(U16).rearrange("p a (t m) -> p a m t", t=PACK),
             wd_raw[:].bitcast(U16).rearrange("p a (m t) -> p a m t", t=PACK),
         )
-        deal_wu(1)
+        gather_gate(0, kib=AT_GATED0)
         hidden(0, 0)
+        deal_wu(1)
         quantise_wg(0, 1)
         quantise_wg(1, 1)
         wd_scale = sb("wd_scale", [P, PASSES, N], U8, tag="wg_bf01")
-        place_scale_rows(wd_scale, rows[64:96, 0:N])
+        place_scale_rows(wd_scale, scale_rows[64:96, 0:N])
         hidden(0, 1)
         load_gate(2, AT_GATE2)
         load_gate(3, AT_GATE3)

@@ -39,7 +39,8 @@ AT_ROUNDED00, AT_WG11 = 60, 60
 AT_WG10 = 68
 AT_GATE1, AT_GATE2, AT_GATE3 = AT_WG10, AT_WG01, AT_WG11
 ACT_AT = {(0, 1, 2): AT_WG01, (0, 1, 3): AT_WG11}
-AT_PAGE = (AT_PAGE0, AT_GATE3, AT_GATED0)
+AT_Z0 = 76
+AT_PAGE = (AT_PAGE0, AT_GATE3, AT_Z0)
 
 
 def tile_list_modp_gsilu_gateP_kernel(
@@ -232,7 +233,9 @@ def tile_list_modp_gsilu_gateP_kernel(
             h_scale[b, half] = sb(f"h_scale{b}{half}", [P, HALF], U8)
             nc.vector.quantize_mx(out=h_codes[b, half][:].bitcast(FP8X4), scales=h_scale[b, half][:], in_=rounded[:])
 
-        y_sb = [sb(f"y_sb{u}", [P, J], F32) for u in range(PACK)]
+        y_sb = {u: sb(f"y_sb{u}", [P, J], F32) for u in range(1, PACK)}
+        z = {u: sb(f"z{u}", [P, J], F32) for u in range(1, PACK)}
+        z[0] = staged("z0", [P, J], F32, AT_Z0)
 
         def down(u, half, bank="y", bufs=2):
             y = psum.tile([P, HALF], F32, name="y", tag=bank, bufs=bufs)
@@ -247,12 +250,14 @@ def tile_list_modp_gsilu_gateP_kernel(
                     start=(a == 0),
                     stop=(a == PASSES - 1),
                 )
-            nc.scalar.copy(y_sb[u][:, HALF * half : HALF * (half + 1)], y[:])
+            cols = slice(HALF * half, HALF * (half + 1))
+            if u == 0:
+                nc.vector.tensor_tensor(z[0][:, cols], y[:], gate[0][:, cols], MULT)
+            else:
+                nc.scalar.copy(y_sb[u][:, cols], y[:])
 
         def scatter(u, j0, j1):
-            nc.vector.tensor_tensor(
-                page[u][:].indirect(offsets[:, j0 // GROUP : j1 // GROUP]), y_sb[u][:, j0:j1], gate[u][:, j0:j1], MULT
-            )
+            nc.vector.tensor_copy(page[u][:].indirect(offsets[:, j0 // GROUP : j1 // GROUP]), z[u][:, j0:j1])
 
         quantise_wg(0, 0)
         load_wg(0, 1, AT_WG01)
@@ -296,6 +301,8 @@ def tile_list_modp_gsilu_gateP_kernel(
             elif u > 0:
                 page[u] = staged(f"page{u}", [P, T], F32, AT_PAGE[u])
                 nc.gpsimd.memset(page[u][:].bitcast(I32), 0)
+            if u > 0:
+                nc.gpsimd.tensor_tensor(z[u][:], y_sb[u][:], gate[u][:], MULT)
             scatter(u, HALF if u == 0 else 0, J)
             queue = nc.scalar if u == last else nc.sync
             queue.dma_start(out_rows[:, PLANE[u], :], page[u][:])

@@ -34,13 +34,18 @@ AT_WU0, AT_PICKED_SCALES, AT_WD = 4, 7.5, 8
 AT_WU1, AT_TAB_WORDS, AT_GATE0 = 12, 14, 20
 AT_WG00, AT_WG01 = 32, 32
 AT_PICKED_WORDS, AT_GATED0 = 40, 44
-AT_PAGE0, AT_TAB_SCALES = 52, 58
+AT_PAGE0 = 52
 AT_ROUNDED00, AT_WG11 = 60, 60
 AT_WG10 = 68
-AT_GATE1, AT_GATE2, AT_GATE3 = AT_WG10, AT_WG01, AT_WG11
+AT_GATE1, AT_GATE2, AT_GATE3 = AT_WG10, 96, AT_WG11
+AT_ROUNDED10 = 96
+AT_H = {(0, 0): AT_GATE0, (0, 1): 78, (1, 0): 80, (1, 1): 82}
+AT_GATED = (AT_GATED0, 76, AT_GATE1, 84)
+AT_WEIGHED1 = 80
+GPSIMD_STEPS = ((1, 0, 0), (1, 0, 1), (1, 0, 2), (1, 1, 1), (1, 1, 2), (1, 1, 3))
+AT_DRAINED = 8
 ACT_AT = {(0, 1, 2): AT_WG01, (0, 1, 3): AT_WG11}
-AT_Z0 = 76
-AT_PAGE = (AT_PAGE0, AT_GATE3, AT_Z0)
+AT_PAGE = (AT_PAGE0, 88, 76)
 
 
 def tile_list_modp_gsilu_gateP_kernel(
@@ -59,19 +64,22 @@ def tile_list_modp_gsilu_gateP_kernel(
         def staged(name, shape, dtype, kib):
             return shared.tile(shape, dtype, name=name, offset=int(1024 * kib), align_bytes=64)
 
+        def bank(name, number):
+            return psum.tile([P, HALF], F32, name=name, offset=2048 * number)
+
         offsets = keep.tile([P, J // GROUP], U16, name="offsets")
         nc.sync.dma_start(offsets[:], offs)
 
-        ts_raw = staged("ts_raw", [P, T], U8, AT_TAB_SCALES)
+        ts_raw = sb("ts_raw", [P, T], U8)
         ws_raw = sb("ws_raw", [P, R], U8)
         nc.sync.dma_start(ts_raw[96:128, :].bitcast(I32), tab_scales.rearrange("a q t -> q a t").bitcast(I32))
         nc.sync.dma_start(ws_raw[96:128, :].bitcast(I32), wu_scales.rearrange("a q r -> q a r").bitcast(I32))
         nc.sync.dma_start(ws_raw[64:96, 0:N].bitcast(I32), wd_scales.rearrange("a q n -> q a n").bitcast(I32))
         warm_in = sb("warm_in", [P, 1], F32)
         nc.vector.memset(warm_in[:], 0)
-        nc.vector.memset(ts_raw[0:96, :].bitcast(I32), 0)
-        nc.vector.memset(ws_raw[0:64, :].bitcast(I32), 0)
-        nc.vector.memset(ws_raw[64:96, N:R].bitcast(I32), 0)
+        nc.gpsimd.memset(ts_raw[0:96, :].bitcast(I32), 0)
+        nc.gpsimd.memset(ws_raw[0:64, :].bitcast(I32), 0)
+        nc.gpsimd.memset(ws_raw[64:96, N:R].bitcast(I32), 0)
 
         wgo_row = sb("wgo_row", [P, J // P], F32)
         nc.sync.dma_start(wgo_row[:], wgo[0].rearrange("(p c) -> p c", p=P))
@@ -81,7 +89,7 @@ def tile_list_modp_gsilu_gateP_kernel(
         nc.scalar.activation(warm_out[:], warm_in[:], SILU)
         wgo_sb = sb("wgo_sb", [P, J], F32)
         for g in range(J // HALF):
-            spread = psum.tile([P, HALF], F32, name="spread", tag="y", bufs=2)
+            spread = bank(f"spread{g}", 6 + g)
             for c in range(PACK):
                 column = wgo_row[:, PACK * g + c : PACK * g + c + 1]
                 nc.tensor.transpose(spread[:, P * c : P * (c + 1)], column.to_broadcast([P, P]), identity[:])
@@ -124,8 +132,10 @@ def tile_list_modp_gsilu_gateP_kernel(
 
         ts_picked = staged("ts_picked", [P, J], U8, AT_PICKED_SCALES)
         nc.vector.tensor_copy(ts_picked[:], ts_raw[:].indirect(offsets[:]))
-        page = {0: staged("page0", [P, T], F32, AT_PAGE[0])}
-        nc.gpsimd.memset(page[0][:].bitcast(I32), 0)
+        page = {}
+        for u in range(2):
+            page[u] = staged(f"page{u}", [P, T], F32, AT_PAGE[u])
+            nc.gpsimd.memset(page[u][:].bitcast(I32), 0)
 
         scale_rows = sb("scale_rows", [P, R + J], U8)
         nc.vector.tensor_copy(
@@ -165,6 +175,8 @@ def tile_list_modp_gsilu_gateP_kernel(
         def quantise_wg(a, b):
             if (a, b) == (0, 0):
                 rounded = staged("wg_bf00", [P, PACK * PASS], BF16, AT_ROUNDED00)
+            elif (a, b) == (1, 0):
+                rounded = staged("wg_bf10", [P, PACK * PASS], BF16, AT_ROUNDED10)
             else:
                 rounded = sb(f"wg_bf{a}{b}", [P, PACK * PASS], BF16)
             dst = rounded[:].rearrange("p (t m i) -> p m i t", t=PACK, i=PACK)
@@ -181,21 +193,27 @@ def tile_list_modp_gsilu_gateP_kernel(
 
         gate = {}
 
-        def gather_gate(u, tag=None, kib=None):
-            gate[u] = sb(f"gate{u}", [P, J], F32, tag=tag) if kib is None else staged(f"gate{u}", [P, J], F32, kib)
-            nc.vector.tensor_tensor(gate[u][:], gate_raw[u][:].indirect(offsets[:]), wgo_sb[:], MULT)
+        def gather_gate(u):
+            gate[u] = staged(f"gate{u}", [P, J], F32, AT_GATED[u])
+            if u == 0:
+                nc.vector.tensor_tensor(gate[u][:], gate_raw[u][:].indirect(offsets[:]), wgo_sb[:], MULT)
+            else:
+                nc.vector.tensor_copy(gate[u][:], gate_raw[u][:].indirect(offsets[:]))
 
         h_codes, h_scale = {}, {}
 
-        def hidden(b, half):
-            if (b, half) == (0, 0):
-                rounded = staged("h_bf00", [P, PACK * HALF], BF16, AT_GATE0)
-            else:
-                rounded = sb(f"h_bf{b}{half}", [P, PACK * HALF], BF16)
+        def hidden(b, half, ahead_of_last=None):
+            rounded = staged(f"h_bf{b}{half}", [P, PACK * HALF], BF16, AT_H[b, half])
             for s in range(HALF // P):
                 j0 = HALF * half + P * s
-                ga = psum.tile([P, PACK * P], F32, name="ga", tag="ga", bufs=3)
-                ub = psum.tile([P, PACK * P], F32, name="ub", tag="ub", bufs=3)
+                step = 8 * b + 4 * half + s
+                if s == 3 and ahead_of_last:
+                    ahead_of_last()
+                ga = bank(f"ga{step}", step % 3)
+                if b == 1 and (b, half, s) not in GPSIMD_STEPS:
+                    ub = bank(f"ub{step}", 6 + half)
+                else:
+                    ub = bank(f"ub{step}", 3 + step % 3)
                 for a in range(PASSES):
                     for t in range(PACK):
                         nc.tensor.matmul_mx(
@@ -218,6 +236,19 @@ def tile_list_modp_gsilu_gateP_kernel(
                             start=(a == 0),
                             stop=(a == PASSES - 1),
                         )
+                if (b, half, s) in GPSIMD_STEPS:
+                    kib = AT_DRAINED + 4 * GPSIMD_STEPS.index((b, half, s))
+                    act = staged(f"act{half}{s}", [P, PACK * P], F32, kib)
+                    ub_sb = staged(f"ub_sb{half}{s}", [P, PACK * P], F32, kib + 2)
+                    walk = "p (c e t) -> p c t e"
+                    nc.scalar.activation(
+                        act[:].rearrange(walk, t=PACK, e=2), ga[:].rearrange("p (t c e) -> p c t e", t=PACK, e=2), SILU
+                    )
+                    nc.scalar.copy(
+                        ub_sb[:].rearrange(walk, t=PACK, e=2), ub[:].rearrange("p (t c e) -> p c t e", t=PACK, e=2)
+                    )
+                    nc.gpsimd.tensor_tensor(rounded[:, PACK * P * s : PACK * P * (s + 1)], ub_sb[:], act[:], MULT)
+                    continue
                 if (b, half, s) in ACT_AT:
                     act = staged(f"act{s}", [P, P // 2, PACK, 2], F32, ACT_AT[b, half, s])
                 else:
@@ -235,10 +266,10 @@ def tile_list_modp_gsilu_gateP_kernel(
 
         y_sb = {u: sb(f"y_sb{u}", [P, J], F32) for u in range(1, PACK)}
         z = {u: sb(f"z{u}", [P, J], F32) for u in range(1, PACK)}
-        z[0] = staged("z0", [P, J], F32, AT_Z0)
+        z[0] = sb("z0", [P, J], F32)
 
-        def down(u, half, bank="y", bufs=2):
-            y = psum.tile([P, HALF], F32, name="y", tag=bank, bufs=bufs)
+        def down(u, half, number):
+            y = bank(f"y{u}{half}", number)
             n0 = P * PLANE[u]
             for a in range(PASSES):
                 nc.tensor.matmul_mx(
@@ -265,12 +296,13 @@ def tile_list_modp_gsilu_gateP_kernel(
         deal_wu(0)
         quantise_wg(1, 0)
         load_gate(1, AT_GATE1)
+        load_gate(2, AT_GATE2)
         wd_codes = sb("wd_codes", [P, PASSES, 2 * N], U8)
         nc.vector.tensor_copy(
             wd_codes[:].bitcast(U16).rearrange("p a (t m) -> p a m t", t=PACK),
             wd_raw[:].bitcast(U16).rearrange("p a (m t) -> p a m t", t=PACK),
         )
-        gather_gate(0, kib=AT_GATED0)
+        gather_gate(0)
         hidden(0, 0)
         deal_wu(1)
         quantise_wg(0, 1)
@@ -278,18 +310,22 @@ def tile_list_modp_gsilu_gateP_kernel(
         wd_scale = sb("wd_scale", [P, PASSES, N], U8, tag="wg_bf01")
         place_scale_rows(wd_scale, scale_rows[64:96, 0:N])
         hidden(0, 1)
-        load_gate(2, AT_GATE2)
         load_gate(3, AT_GATE3)
         gather_gate(1)
-        hidden(1, 0)
         gather_gate(2)
+        hidden(1, 0)
+
+
+        def first_scatter():
+            down(0, 0, 13 % 3)
+            scatter(0, 0, HALF)
+
+        hidden(1, 1, first_scatter)
+        for u in range(1, PACK):
+            down(u, 0, (6, 7, 2)[u - 1])
+        gather_gate(3)
         for u in range(PACK):
-            down(u, 0)
-        scatter(0, 0, HALF)
-        hidden(1, 1)
-        gather_gate(3, tag="h_bf11")
-        for u in range(PACK):
-            down(u, 1, ("ga", "ub")[u % 2], 3)
+            down(u, 1, (0, 3, 4, 5)[u])
 
         pieces = list(zip(EDGES[:-1], EDGES[1:]))
         out_bf = sb("out_bf", [P, T, PACK], BF16, tag="h_codes11")
@@ -298,11 +334,16 @@ def tile_list_modp_gsilu_gateP_kernel(
         for u in range(PACK):
             if u == last:
                 page[u] = page[0]
-            elif u > 0:
+            elif u > 1:
                 page[u] = staged(f"page{u}", [P, T], F32, AT_PAGE[u])
                 nc.gpsimd.memset(page[u][:].bitcast(I32), 0)
             if u > 0:
-                nc.gpsimd.tensor_tensor(z[u][:], y_sb[u][:], gate[u][:], MULT)
+                if u == 1:
+                    weighed = staged("weighed1", [P, J], F32, AT_WEIGHED1)
+                else:
+                    weighed = sb(f"weighed{u}", [P, J], F32, tag=f"y_sb{u - 1}")
+                nc.gpsimd.tensor_tensor(weighed[:], gate[u][:], wgo_sb[:], MULT)
+                nc.gpsimd.tensor_tensor(z[u][:], y_sb[u][:], weighed[:], MULT)
             scatter(u, HALF if u == 0 else 0, J)
             queue = nc.scalar if u == last else nc.sync
             queue.dma_start(out_rows[:, PLANE[u], :], page[u][:])

@@ -30,22 +30,22 @@ PLANE = (2, 0, 1, 3)
 EDGES = (0, 512, 1024, 1536, 1792, 2048)
 VECTOR_PIECES = 2
 
-AT_WU0, AT_PICKED_SCALES, AT_WD = 4, 7.5, 8
+AT_WU0, AT_PICKED_SCALES, AT_WD = 104, 103.5, 40
 AT_WU1, AT_TAB_WORDS, AT_GATE0 = 12, 14, 20
 AT_WG00, AT_WG01 = 32, 32
 AT_PICKED_WORDS, AT_GATED0 = 40, 44
 AT_PAGE0 = 52
 AT_ROUNDED00, AT_WG11 = 60, 60
 AT_WG10 = 68
-AT_GATE1, AT_GATE2, AT_GATE3 = AT_WG10, 96, AT_WG11
-AT_ROUNDED10 = 96
+AT_GATE1, AT_GATE2, AT_GATE3 = AT_WG10, 88, AT_WG11
+AT_ROUNDED10 = 88
 AT_H = {(0, 0): AT_GATE0, (0, 1): 78, (1, 0): 80, (1, 1): 82}
 AT_GATED = (AT_GATED0, 76, AT_GATE1, 84)
 AT_WEIGHED1 = 80
 GPSIMD_STEPS = ((1, 0, 0), (1, 0, 1), (1, 0, 2), (1, 1, 1), (1, 1, 2), (1, 1, 3))
-AT_DRAINED = 8
+AT_DRAINED = 4
 ACT_AT = {(0, 1, 2): AT_WG01, (0, 1, 3): AT_WG11}
-AT_PAGE = (AT_PAGE0, 88, 76)
+AT_PAGE = (AT_PAGE0, 96, 76)
 
 
 def tile_list_modp_gsilu_gateP_kernel(
@@ -77,9 +77,9 @@ def tile_list_modp_gsilu_gateP_kernel(
         nc.sync.dma_start(ws_raw[64:96, 0:N].bitcast(I32), wd_scales.rearrange("a q n -> q a n").bitcast(I32))
         warm_in = sb("warm_in", [P, 1], F32)
         nc.vector.memset(warm_in[:], 0)
-        nc.gpsimd.memset(ts_raw[0:96, :].bitcast(I32), 0)
-        nc.gpsimd.memset(ws_raw[0:64, :].bitcast(I32), 0)
-        nc.gpsimd.memset(ws_raw[64:96, N:R].bitcast(I32), 0)
+        nc.vector.memset(ts_raw[0:96, :].bitcast(I32), 0)
+        nc.vector.memset(ws_raw[0:64, :].bitcast(I32), 0)
+        nc.vector.memset(ws_raw[64:96, N:R].bitcast(I32), 0)
 
         wgo_row = sb("wgo_row", [P, J // P], F32)
         nc.sync.dma_start(wgo_row[:], wgo[0].rearrange("(p c) -> p c", p=P))
@@ -133,9 +133,12 @@ def tile_list_modp_gsilu_gateP_kernel(
         ts_picked = staged("ts_picked", [P, J], U8, AT_PICKED_SCALES)
         nc.vector.tensor_copy(ts_picked[:], ts_raw[:].indirect(offsets[:]))
         page = {}
-        for u in range(2):
+
+        def zero_page(u):
             page[u] = staged(f"page{u}", [P, T], F32, AT_PAGE[u])
             nc.gpsimd.memset(page[u][:].bitcast(I32), 0)
+
+        zero_page(0)
 
         scale_rows = sb("scale_rows", [P, R + J], U8)
         nc.vector.tensor_copy(
@@ -147,8 +150,7 @@ def tile_list_modp_gsilu_gateP_kernel(
         place_scale_rows(placed, scale_rows[96:128, :])
         wu_scale, tab_scale = placed[:, :, 0:R], placed[:, :, R:]
         load_wu(0)
-        wd_raw = staged("wd_raw", [P, PASSES, 2 * N], U8, AT_WD)
-        nc.sync.dma_start(wd_raw[:].bitcast(I32), wd_words.rearrange("a p n -> p a n").bitcast(I32))
+        zero_page(1)
 
         tab_picked = staged("tab_picked", [P, J], I32, AT_PICKED_WORDS)
         for j0 in range(0, J, HALF):
@@ -160,6 +162,9 @@ def tile_list_modp_gsilu_gateP_kernel(
         for half in range(J // HALF):
             words = tab_picked[:, HALF * half : HALF * (half + 1)].bitcast(U16)
             nc.vector.tensor_copy(tab_codes[half][:].bitcast(U16), words.rearrange("p (j a) -> p a j", a=PASSES))
+
+        wd_raw = staged("wd_raw", [P, PASSES, 2 * N], U8, AT_WD)
+        nc.sync.dma_start(wd_raw[:].bitcast(I32), wd_words.rearrange("a p n -> p a n").bitcast(I32))
 
         wu_codes = {}
 
@@ -182,8 +187,10 @@ def tile_list_modp_gsilu_gateP_kernel(
             dst = rounded[:].rearrange("p (t m i) -> p m i t", t=PACK, i=PACK)
             src = wg_raw[a, b][:].rearrange("p i (m t) -> p m i t", t=PACK)
             nc.scalar.copy(dst[:, 0 : P // 2], src[:, 0 : P // 2])
-            copy = nc.vector.tensor_copy if (a, b) == (1, 1) else nc.scalar.copy
-            copy(dst[:, P // 2 : P], src[:, P // 2 : P])
+            if (a, b) == (1, 1):
+                nc.vector.tensor_copy(dst[:, P // 2 : P], src[:, P // 2 : P])
+            else:
+                nc.scalar.copy(dst[:, P // 2 : P], src[:, P // 2 : P])
             if (a, b) == (1, 0):
                 wg_codes[a, b] = staged("wg_codes10", [P, PASS], U32, AT_WU0)
             else:
@@ -297,11 +304,6 @@ def tile_list_modp_gsilu_gateP_kernel(
         quantise_wg(1, 0)
         load_gate(1, AT_GATE1)
         load_gate(2, AT_GATE2)
-        wd_codes = sb("wd_codes", [P, PASSES, 2 * N], U8)
-        nc.vector.tensor_copy(
-            wd_codes[:].bitcast(U16).rearrange("p a (t m) -> p a m t", t=PACK),
-            wd_raw[:].bitcast(U16).rearrange("p a (m t) -> p a m t", t=PACK),
-        )
         gather_gate(0)
         hidden(0, 0)
         deal_wu(1)
@@ -310,6 +312,11 @@ def tile_list_modp_gsilu_gateP_kernel(
         wd_scale = sb("wd_scale", [P, PASSES, N], U8, tag="wg_bf01")
         place_scale_rows(wd_scale, scale_rows[64:96, 0:N])
         hidden(0, 1)
+        wd_codes = sb("wd_codes", [P, PASSES, 2 * N], U8, tag="wg_bf11")
+        nc.scalar.copy(
+            wd_codes[:].bitcast(U16).rearrange("p a (t m) -> p a m t", t=PACK),
+            wd_raw[:].bitcast(U16).rearrange("p a (m t) -> p a m t", t=PACK),
+        )
         load_gate(3, AT_GATE3)
         gather_gate(1)
         gather_gate(2)
@@ -335,8 +342,7 @@ def tile_list_modp_gsilu_gateP_kernel(
             if u == last:
                 page[u] = page[0]
             elif u > 1:
-                page[u] = staged(f"page{u}", [P, T], F32, AT_PAGE[u])
-                nc.gpsimd.memset(page[u][:].bitcast(I32), 0)
+                zero_page(u)
             if u > 0:
                 if u == 1:
                     weighed = staged("weighed1", [P, J], F32, AT_WEIGHED1)

@@ -30,22 +30,18 @@ PLANE = (2, 0, 1, 3)
 EDGES = (0, 512, 1024, 1536, 1792, 2048)
 VECTOR_PIECES = 2
 
-AT_WU0, AT_PICKED_SCALES, AT_WD = 104, 103.5, 40
-AT_WU1, AT_TAB_WORDS, AT_GATE0 = 12, 14, 20
-AT_WG00, AT_WG01 = 32, 32
-AT_PICKED_WORDS, AT_GATED0 = 40, 44
-AT_PAGE0 = 52
-AT_ROUNDED00, AT_WG11 = 60, 60
-AT_WG10 = 68
-AT_GATE1, AT_GATE2, AT_GATE3 = AT_WG10, 88, AT_WG11
-AT_ROUNDED10 = 88
-AT_H = {(0, 0): AT_GATE0, (0, 1): 78, (1, 0): 80, (1, 1): 82}
-AT_GATED = (AT_GATED0, 76, AT_GATE1, 84)
-AT_WEIGHED1 = 80
-GPSIMD_STEPS = ((1, 0, 0), (1, 0, 1), (1, 0, 2), (1, 1, 1), (1, 1, 2), (1, 1, 3))
-AT_DRAINED = 4
+AT_DRAINED, AT_TAB_WORDS, AT_PICKED_WORDS = 0, 0, 8
+AT_WG10, AT_WD, AT_GATE1 = 24, 28, 30
+AT_WG01, AT_WG00, AT_WU1 = 38, 44, 46
+AT_WG11, AT_GATE3, AT_ROUNDED00 = 50, 50, 52
+AT_GATE2, AT_ROUNDED10 = 82, 82
+AT_PICKED_SCALES, AT_WU0, AT_WEIGHT_SCALES, AT_GATE0 = 97.5, 98, 101.5, 102
+AT_H = {(0, 0): AT_GATE0, (0, 1): 72, (1, 0): 74, (1, 1): 76}
+AT_GATED = (66, 70, AT_GATE1, 78)
+AT_WEIGHED1 = 74
+AT_PAGE = (58, 90, 70)
 ACT_AT = {(0, 1, 2): AT_WG01, (0, 1, 3): AT_WG11}
-AT_PAGE = (AT_PAGE0, 96, 76)
+GPSIMD_STEPS = ((1, 0, 0), (1, 0, 1), (1, 0, 2), (1, 1, 1), (1, 1, 2), (1, 1, 3))
 
 
 def tile_list_modp_gsilu_gateP_kernel(
@@ -71,7 +67,7 @@ def tile_list_modp_gsilu_gateP_kernel(
         nc.sync.dma_start(offsets[:], offs)
 
         ts_raw = sb("ts_raw", [P, T], U8)
-        ws_raw = sb("ws_raw", [P, R], U8)
+        ws_raw = staged("ws_raw", [P, R], U8, AT_WEIGHT_SCALES)
         nc.sync.dma_start(ts_raw[96:128, :].bitcast(I32), tab_scales.rearrange("a q t -> q a t").bitcast(I32))
         nc.sync.dma_start(ws_raw[96:128, :].bitcast(I32), wu_scales.rearrange("a q r -> q a r").bitcast(I32))
         nc.sync.dma_start(ws_raw[64:96, 0:N].bitcast(I32), wd_scales.rearrange("a q n -> q a n").bitcast(I32))
@@ -141,7 +137,7 @@ def tile_list_modp_gsilu_gateP_kernel(
         zero_page(0)
 
         scale_rows = sb("scale_rows", [P, R + J], U8)
-        nc.vector.tensor_copy(
+        nc.gpsimd.tensor_copy(
             scale_rows[:, 0:R].rearrange("p (b t m) -> p b t m", b=R // PASS, t=PACK),
             ws_raw[:].rearrange("p (b m t) -> p b t m", b=R // PASS, t=PACK),
         )
@@ -157,23 +153,26 @@ def tile_list_modp_gsilu_gateP_kernel(
             listed = tab_raw[:].bitcast(U32).indirect(offsets[:, j0 // GROUP : (j0 + HALF) // GROUP])
             nc.vector.tensor_copy(tab_picked[:, j0 : j0 + HALF].bitcast(U32), listed)
         load_gate(0, AT_GATE0)
-        load_wu(1)
         tab_codes = [sb(f"tab_codes{half}", [P, PASSES, 2 * HALF], U8) for half in range(J // HALF)]
         for half in range(J // HALF):
             words = tab_picked[:, HALF * half : HALF * (half + 1)].bitcast(U16)
             nc.vector.tensor_copy(tab_codes[half][:].bitcast(U16), words.rearrange("p (j a) -> p a j", a=PASSES))
 
-        wd_raw = staged("wd_raw", [P, PASSES, 2 * N], U8, AT_WD)
-        nc.sync.dma_start(wd_raw[:].bitcast(I32), wd_words.rearrange("a p n -> p a n").bitcast(I32))
-
         wu_codes = {}
 
         def deal_wu(b):
-            wu_codes[b] = sb(f"wu_codes{b}", [P, PASSES, PASS], I32)
-            nc.vector.tensor_copy(
-                wu_codes[b][:].rearrange("p a (t m) -> p a m t", t=PACK),
-                wu_raw[b][:].rearrange("p a (m t) -> p a m t", t=PACK),
-            )
+            if b == 0:
+                wu_codes[b] = sb("wu_codes0", [P, PASSES, PASS], I32)
+                nc.vector.tensor_copy(
+                    wu_codes[b][:].rearrange("p a (t m) -> p a m t", t=PACK),
+                    wu_raw[b][:].rearrange("p a (m t) -> p a m t", t=PACK),
+                )
+            else:
+                wu_codes[b] = staged("wu_codes1", [P, PASSES, PASS], I32, 106)
+                nc.gpsimd.tensor_copy(
+                    wu_codes[b][:].rearrange("p a (t m) -> p a t m", t=PACK),
+                    wu_raw[b][:].rearrange("p a (m t) -> p a t m", t=PACK),
+                )
 
         wg_codes, wg_scale = {}, {}
 
@@ -182,12 +181,14 @@ def tile_list_modp_gsilu_gateP_kernel(
                 rounded = staged("wg_bf00", [P, PACK * PASS], BF16, AT_ROUNDED00)
             elif (a, b) == (1, 0):
                 rounded = staged("wg_bf10", [P, PACK * PASS], BF16, AT_ROUNDED10)
+            elif (a, b) == (1, 1):
+                rounded = staged("wg_bf11", [P, PACK * PASS], BF16, 110)
             else:
                 rounded = sb(f"wg_bf{a}{b}", [P, PACK * PASS], BF16)
             dst = rounded[:].rearrange("p (t m i) -> p m i t", t=PACK, i=PACK)
             src = wg_raw[a, b][:].rearrange("p i (m t) -> p m i t", t=PACK)
             nc.scalar.copy(dst[:, 0 : P // 2], src[:, 0 : P // 2])
-            if (a, b) == (1, 1):
+            if a == 1:
                 nc.vector.tensor_copy(dst[:, P // 2 : P], src[:, P // 2 : P])
             else:
                 nc.scalar.copy(dst[:, P // 2 : P], src[:, P // 2 : P])
@@ -217,10 +218,7 @@ def tile_list_modp_gsilu_gateP_kernel(
                 if s == 3 and ahead_of_last:
                     ahead_of_last()
                 ga = bank(f"ga{step}", step % 3)
-                if b == 1 and (b, half, s) not in GPSIMD_STEPS:
-                    ub = bank(f"ub{step}", 6 + half)
-                else:
-                    ub = bank(f"ub{step}", 3 + step % 3)
+                ub = bank(f"ub{step}", 3 + step % 5)
                 for a in range(PASSES):
                     for t in range(PACK):
                         nc.tensor.matmul_mx(
@@ -298,21 +296,24 @@ def tile_list_modp_gsilu_gateP_kernel(
             nc.vector.tensor_copy(page[u][:].indirect(offsets[:, j0 // GROUP : j1 // GROUP]), z[u][:, j0:j1])
 
         quantise_wg(0, 0)
+        load_wu(1)
         load_wg(0, 1, AT_WG01)
         load_wg(1, 1, AT_WG11)
         deal_wu(0)
         quantise_wg(1, 0)
+        wd_raw = staged("wd_raw", [P, PASSES, 2 * N], U8, AT_WD)
+        nc.sync.dma_start(wd_raw[:].bitcast(I32), wd_words.rearrange("a p n -> p a n").bitcast(I32))
         load_gate(1, AT_GATE1)
         load_gate(2, AT_GATE2)
         gather_gate(0)
-        hidden(0, 0)
         deal_wu(1)
+        hidden(0, 0)
         quantise_wg(0, 1)
         quantise_wg(1, 1)
         wd_scale = sb("wd_scale", [P, PASSES, N], U8, tag="wg_bf01")
         place_scale_rows(wd_scale, scale_rows[64:96, 0:N])
         hidden(0, 1)
-        wd_codes = sb("wd_codes", [P, PASSES, 2 * N], U8, tag="wg_bf11")
+        wd_codes = staged("wd_codes", [P, PASSES, 2 * N], U8, 110)
         nc.scalar.copy(
             wd_codes[:].bitcast(U16).rearrange("p a (t m) -> p a m t", t=PACK),
             wd_raw[:].bitcast(U16).rearrange("p a (m t) -> p a m t", t=PACK),
@@ -324,15 +325,15 @@ def tile_list_modp_gsilu_gateP_kernel(
 
 
         def first_scatter():
-            down(0, 0, 13 % 3)
+            down(0, 0, 3 + 13 % 5)
             scatter(0, 0, HALF)
 
         hidden(1, 1, first_scatter)
         for u in range(1, PACK):
-            down(u, 0, (6, 7, 2)[u - 1])
+            down(u, 0, (4, 5, 7)[u - 1])
         gather_gate(3)
         for u in range(PACK):
-            down(u, 1, (0, 3, 4, 5)[u])
+            down(u, 1, (1, 2, 0, 3)[u])
 
         pieces = list(zip(EDGES[:-1], EDGES[1:]))
         out_bf = sb("out_bf", [P, T, PACK], BF16, tag="h_codes11")

@@ -30,18 +30,26 @@ PLANE = (2, 0, 1, 3)
 EDGES = (0, 512, 1024, 1536, 1792, 2048)
 VECTOR_PIECES = 2
 
-AT_DRAINED, AT_TAB_WORDS, AT_PICKED_WORDS = 0, 0, 8
+AT_TAB_WORDS, AT_PICKED_WORDS = 0, 8
 AT_WG10, AT_WD, AT_GATE1 = 24, 28, 30
 AT_WG01, AT_WG00, AT_WU1 = 38, 44, 46
-AT_WG11, AT_GATE3, AT_ROUNDED00 = 50, 50, 52
-AT_GATE2, AT_ROUNDED10 = 82, 82
-AT_PICKED_SCALES, AT_WU0, AT_WEIGHT_SCALES, AT_GATE0 = 97.5, 98, 101.5, 102
-AT_H = {(0, 0): AT_GATE0, (0, 1): 72, (1, 0): 74, (1, 1): 76}
-AT_GATED = (66, 70, AT_GATE1, 78)
-AT_WEIGHED1 = 74
-AT_PAGE = (58, 90, 70)
-ACT_AT = {(0, 1, 2): AT_WG01, (0, 1, 3): AT_WG11}
-GPSIMD_STEPS = ((1, 0, 0), (1, 0, 1), (1, 0, 2), (1, 1, 1), (1, 1, 2), (1, 1, 3))
+AT_WG11, AT_ROUNDED00 = 50, 52
+AT_GATE3 = AT_WG11
+AT_PAGE0 = 58
+AT_ROUNDED11, AT_WD_CODES = 86, 86
+AT_PAGE1, AT_PICKED_SCALES, AT_WU0 = 90, 97.5, 98
+AT_WEIGHT_SCALES, AT_GATE0 = 101.5, 102
+AT_WU1_CODES = AT_GATE0 + 4
+AT_PAGE2, AT_ROUNDED10, AT_GATE2 = 110, 116, 118
+AT_PAGE = (AT_PAGE0, AT_PAGE1, AT_PAGE2)
+
+RUNS = ((0, 4, AT_GATE0), (4, 7, 73.75), (7, 9, 76.5), (9, 12, 78.25), (12, 16, 81))
+AT_GATED = (66, 70, 74, 82)
+AT_WEIGHED1 = 78
+GPSIMD_STEPS = {7: AT_WG11, 8: 0, 9: 4, 10: 8, 13: 12, 14: 16, 15: 20}
+ACT_ON_WG01 = 6
+
+GA_BANKS, UB_BANKS = 3, 5
 
 
 def tile_list_modp_gsilu_gateP_kernel(
@@ -62,6 +70,12 @@ def tile_list_modp_gsilu_gateP_kernel(
 
         def bank(name, number):
             return psum.tile([P, HALF], F32, name=name, offset=2048 * number)
+
+        def ga_bank(step):
+            return step % GA_BANKS
+
+        def ub_bank(step):
+            return GA_BANKS + step % UB_BANKS
 
         offsets = keep.tile([P, J // GROUP], U16, name="offsets")
         nc.sync.dma_start(offsets[:], offs)
@@ -85,7 +99,7 @@ def tile_list_modp_gsilu_gateP_kernel(
         nc.scalar.activation(warm_out[:], warm_in[:], SILU)
         wgo_sb = sb("wgo_sb", [P, J], F32)
         for g in range(J // HALF):
-            spread = bank(f"spread{g}", 6 + g)
+            spread = bank(f"spread{g}", ub_bank(3 + g))
             for c in range(PACK):
                 column = wgo_row[:, PACK * g + c : PACK * g + c + 1]
                 nc.tensor.transpose(spread[:, P * c : P * (c + 1)], column.to_broadcast([P, P]), identity[:])
@@ -163,35 +177,28 @@ def tile_list_modp_gsilu_gateP_kernel(
         def deal_wu(b):
             if b == 0:
                 wu_codes[b] = sb("wu_codes0", [P, PASSES, PASS], I32)
-                nc.vector.tensor_copy(
-                    wu_codes[b][:].rearrange("p a (t m) -> p a m t", t=PACK),
-                    wu_raw[b][:].rearrange("p a (m t) -> p a m t", t=PACK),
-                )
+                copy, walk = nc.vector.tensor_copy, "p a m t"
             else:
-                wu_codes[b] = staged("wu_codes1", [P, PASSES, PASS], I32, 106)
-                nc.gpsimd.tensor_copy(
-                    wu_codes[b][:].rearrange("p a (t m) -> p a t m", t=PACK),
-                    wu_raw[b][:].rearrange("p a (m t) -> p a t m", t=PACK),
-                )
+                wu_codes[b] = staged("wu_codes1", [P, PASSES, PASS], I32, AT_WU1_CODES)
+                copy, walk = nc.gpsimd.tensor_copy, "p a t m"
+            copy(
+                wu_codes[b][:].rearrange("p a (t m) -> " + walk, t=PACK),
+                wu_raw[b][:].rearrange("p a (m t) -> " + walk, t=PACK),
+            )
 
         wg_codes, wg_scale = {}, {}
 
         def quantise_wg(a, b):
-            if (a, b) == (0, 0):
-                rounded = staged("wg_bf00", [P, PACK * PASS], BF16, AT_ROUNDED00)
-            elif (a, b) == (1, 0):
-                rounded = staged("wg_bf10", [P, PACK * PASS], BF16, AT_ROUNDED10)
-            elif (a, b) == (1, 1):
-                rounded = staged("wg_bf11", [P, PACK * PASS], BF16, 110)
+            if (a, b) == (0, 1):
+                rounded = sb("wg_bf01", [P, PACK * PASS], BF16)
             else:
-                rounded = sb(f"wg_bf{a}{b}", [P, PACK * PASS], BF16)
+                kib = {(0, 0): AT_ROUNDED00, (1, 0): AT_ROUNDED10, (1, 1): AT_ROUNDED11}[a, b]
+                rounded = staged(f"wg_bf{a}{b}", [P, PACK * PASS], BF16, kib)
             dst = rounded[:].rearrange("p (t m i) -> p m i t", t=PACK, i=PACK)
             src = wg_raw[a, b][:].rearrange("p i (m t) -> p m i t", t=PACK)
             nc.scalar.copy(dst[:, 0 : P // 2], src[:, 0 : P // 2])
-            if a == 1:
-                nc.vector.tensor_copy(dst[:, P // 2 : P], src[:, P // 2 : P])
-            else:
-                nc.scalar.copy(dst[:, P // 2 : P], src[:, P // 2 : P])
+            copy = nc.vector.tensor_copy if a == 1 else nc.scalar.copy
+            copy(dst[:, P // 2 : P], src[:, P // 2 : P])
             if (a, b) == (1, 0):
                 wg_codes[a, b] = staged("wg_codes10", [P, PASS], U32, AT_WU0)
             else:
@@ -208,17 +215,20 @@ def tile_list_modp_gsilu_gateP_kernel(
             else:
                 nc.vector.tensor_copy(gate[u][:], gate_raw[u][:].indirect(offsets[:]))
 
-        h_codes, h_scale = {}, {}
+        h_codes = sb("h_codes", [P, PASSES * J], U32)
+        h_scale = sb("h_scale", [P, PASSES * J], U8)
 
-        def hidden(b, half, ahead_of_last=None):
-            rounded = staged(f"h_bf{b}{half}", [P, PACK * HALF], BF16, AT_H[b, half])
-            for s in range(HALF // P):
-                j0 = HALF * half + P * s
-                step = 8 * b + 4 * half + s
-                if s == 3 and ahead_of_last:
+        def hidden(run, ahead_of_last=None):
+            first, end, kib = RUNS[run]
+            rounded = staged(f"h_bf{run}", [P, PACK * P * (end - first)], BF16, kib)
+            for step in range(first, end):
+                b, j0 = divmod(P * step, J)
+                half, s = j0 // HALF, j0 % HALF // P
+                out = rounded[:, PACK * P * (step - first) : PACK * P * (step - first + 1)]
+                if step == end - 1 and ahead_of_last:
                     ahead_of_last()
-                ga = bank(f"ga{step}", step % 3)
-                ub = bank(f"ub{step}", 3 + step % 5)
+                ga = bank(f"ga{step}", ga_bank(step))
+                ub = bank(f"ub{step}", ub_bank(step))
                 for a in range(PASSES):
                     for t in range(PACK):
                         nc.tensor.matmul_mx(
@@ -241,37 +251,27 @@ def tile_list_modp_gsilu_gateP_kernel(
                             start=(a == 0),
                             stop=(a == PASSES - 1),
                         )
-                if (b, half, s) in GPSIMD_STEPS:
-                    kib = AT_DRAINED + 4 * GPSIMD_STEPS.index((b, half, s))
-                    act = staged(f"act{half}{s}", [P, PACK * P], F32, kib)
-                    ub_sb = staged(f"ub_sb{half}{s}", [P, PACK * P], F32, kib + 2)
-                    walk = "p (c e t) -> p c t e"
-                    nc.scalar.activation(
-                        act[:].rearrange(walk, t=PACK, e=2), ga[:].rearrange("p (t c e) -> p c t e", t=PACK, e=2), SILU
-                    )
-                    nc.scalar.copy(
-                        ub_sb[:].rearrange(walk, t=PACK, e=2), ub[:].rearrange("p (t c e) -> p c t e", t=PACK, e=2)
-                    )
-                    nc.gpsimd.tensor_tensor(rounded[:, PACK * P * s : PACK * P * (s + 1)], ub_sb[:], act[:], MULT)
-                    continue
-                if (b, half, s) in ACT_AT:
-                    act = staged(f"act{s}", [P, P // 2, PACK, 2], F32, ACT_AT[b, half, s])
+                ga_walk = ga[:].rearrange("p (t c e) -> p c t e", t=PACK, e=2)
+                ub_walk = ub[:].rearrange("p (t c e) -> p c t e", t=PACK, e=2)
+                interleaved = "p (c e t) -> p c t e"
+                if step in GPSIMD_STEPS:
+                    act = staged(f"act{step}", [P, PACK * P], F32, GPSIMD_STEPS[step])
+                    ub_sb = staged(f"ub_sb{step}", [P, PACK * P], F32, GPSIMD_STEPS[step] + 2)
+                    nc.scalar.activation(act[:].rearrange(interleaved, t=PACK, e=2), ga_walk, SILU)
+                    nc.scalar.copy(ub_sb[:].rearrange(interleaved, t=PACK, e=2), ub_walk)
+                    nc.gpsimd.tensor_tensor(out, ub_sb[:], act[:], MULT)
                 else:
-                    act = ring.tile([P, P // 2, PACK, 2], F32, name="act")
-                nc.scalar.activation(act[:], ga[:].rearrange("p (t c e) -> p c t e", t=PACK, e=2), SILU)
-                nc.vector.tensor_tensor(
-                    rounded[:, PACK * P * s : PACK * P * (s + 1)].rearrange("p (c e t) -> p c t e", t=PACK, e=2),
-                    ub[:].rearrange("p (t c e) -> p c t e", t=PACK, e=2),
-                    act[:],
-                    MULT,
-                )
-            h_codes[b, half] = sb(f"h_codes{b}{half}", [P, HALF], U32)
-            h_scale[b, half] = sb(f"h_scale{b}{half}", [P, HALF], U8)
-            nc.vector.quantize_mx(out=h_codes[b, half][:].bitcast(FP8X4), scales=h_scale[b, half][:], in_=rounded[:])
+                    if step == ACT_ON_WG01:
+                        act = staged(f"act{step}", [P, P // 2, PACK, 2], F32, AT_WG01)
+                    else:
+                        act = ring.tile([P, P // 2, PACK, 2], F32, name="act")
+                    nc.scalar.activation(act[:], ga_walk, SILU)
+                    nc.vector.tensor_tensor(out.rearrange(interleaved, t=PACK, e=2), ub_walk, act[:], MULT)
+            words = slice(P * first, P * end)
+            nc.vector.quantize_mx(out=h_codes[:, words].bitcast(FP8X4), scales=h_scale[:, words], in_=rounded[:])
 
         y_sb = {u: sb(f"y_sb{u}", [P, J], F32) for u in range(1, PACK)}
-        z = {u: sb(f"z{u}", [P, J], F32) for u in range(1, PACK)}
-        z[0] = sb("z0", [P, J], F32)
+        z = {u: sb(f"z{u}", [P, J], F32) for u in range(PACK)}
 
         def down(u, half, number):
             y = bank(f"y{u}{half}", number)
@@ -281,8 +281,8 @@ def tile_list_modp_gsilu_gateP_kernel(
                     out=y[:],
                     lhsT=wd_codes[:, a, 2 * n0 : 2 * (n0 + P)].bitcast(FP4X4),
                     lhsT_scale=wd_scale[:, a, n0 : n0 + P],
-                    rhs=h_codes[a, half][:].bitcast(FP8X4),
-                    rhs_scale=h_scale[a, half][:],
+                    rhs=h_codes[:, J * a + HALF * half : J * a + HALF * (half + 1)].bitcast(FP8X4),
+                    rhs_scale=h_scale[:, J * a + HALF * half : J * a + HALF * (half + 1)],
                     start=(a == 0),
                     stop=(a == PASSES - 1),
                 )
@@ -305,45 +305,44 @@ def tile_list_modp_gsilu_gateP_kernel(
         nc.sync.dma_start(wd_raw[:].bitcast(I32), wd_words.rearrange("a p n -> p a n").bitcast(I32))
         load_gate(1, AT_GATE1)
         load_gate(2, AT_GATE2)
+        zero_page(2)
         gather_gate(0)
         deal_wu(1)
-        hidden(0, 0)
+        hidden(0)
         quantise_wg(0, 1)
         quantise_wg(1, 1)
         wd_scale = sb("wd_scale", [P, PASSES, N], U8, tag="wg_bf01")
         place_scale_rows(wd_scale, scale_rows[64:96, 0:N])
-        hidden(0, 1)
-        wd_codes = staged("wd_codes", [P, PASSES, 2 * N], U8, 110)
+        hidden(1)
+        gather_gate(1)
+        hidden(2)
+        wd_codes = staged("wd_codes", [P, PASSES, 2 * N], U8, AT_WD_CODES)
         nc.scalar.copy(
             wd_codes[:].bitcast(U16).rearrange("p a (t m) -> p a m t", t=PACK),
             wd_raw[:].bitcast(U16).rearrange("p a (m t) -> p a m t", t=PACK),
         )
         load_gate(3, AT_GATE3)
-        gather_gate(1)
         gather_gate(2)
-        hidden(1, 0)
-
+        hidden(3)
 
         def first_scatter():
-            down(0, 0, 3 + 13 % 5)
+            down(0, 0, ub_bank(13))
             scatter(0, 0, HALF)
 
-        hidden(1, 1, first_scatter)
-        for u in range(1, PACK):
-            down(u, 0, (4, 5, 7)[u - 1])
+        hidden(4, first_scatter)
+        for u, step in zip(range(1, PACK), (11, 12, 14)):
+            down(u, 0, ub_bank(step))
         gather_gate(3)
-        for u in range(PACK):
-            down(u, 1, (1, 2, 0, 3)[u])
+        for u, number in enumerate((ga_bank(13), ga_bank(14), ga_bank(15), ub_bank(15))):
+            down(u, 1, number)
 
         pieces = list(zip(EDGES[:-1], EDGES[1:]))
-        out_bf = sb("out_bf", [P, T, PACK], BF16, tag="h_codes11")
+        out_bf = sb("out_bf", [P, T, PACK], BF16, tag="h_codes")
         out_rows = out_0.rearrange("(p t) c -> p t c", t=PACK)
         last = PACK - 1
         for u in range(PACK):
             if u == last:
                 page[u] = page[0]
-            elif u > 1:
-                zero_page(u)
             if u > 0:
                 if u == 1:
                     weighed = staged("weighed1", [P, J], F32, AT_WEIGHED1)

@@ -85,8 +85,6 @@ def tile_list_modp_gsilu_gateP_kernel(
         nc.sync.dma_start(ts_raw[96:128, :].bitcast(I32), tab_scales.rearrange("a q t -> q a t").bitcast(I32))
         nc.sync.dma_start(ws_raw[96:128, :].bitcast(I32), wu_scales.rearrange("a q r -> q a r").bitcast(I32))
         nc.sync.dma_start(ws_raw[64:96, 0:N].bitcast(I32), wd_scales.rearrange("a q n -> q a n").bitcast(I32))
-        warm_in = sb("warm_in", [P, 1], F32)
-        nc.vector.memset(warm_in[:], 0)
         nc.vector.memset(ts_raw[0:96, :].bitcast(I32), 0)
         nc.vector.memset(ws_raw[0:64, :].bitcast(I32), 0)
         nc.vector.memset(ws_raw[64:96, N:R].bitcast(I32), 0)
@@ -95,8 +93,6 @@ def tile_list_modp_gsilu_gateP_kernel(
         nc.sync.dma_start(wgo_row[:], wgo[0].rearrange("(p c) -> p c", p=P))
         identity = sb("identity", [P, P], F32)
         make_identity(nc, identity[:])
-        warm_out = sb("warm_out", [P, 1], F32)
-        nc.scalar.activation(warm_out[:], warm_in[:], SILU)
         wgo_sb = sb("wgo_sb", [P, J], F32)
         for g in range(J // HALF):
             spread = bank(f"spread{g}", ub_bank(3 + g))

@@ -173,14 +173,16 @@ def tile_list_modp_gsilu_gateP_kernel(
         def deal_wu(b):
             if b == 0:
                 wu_codes[b] = sb("wu_codes0", [P, PASSES, PASS], I32)
-                copy, walk = nc.vector.tensor_copy, "p a m t"
+                nc.vector.tensor_copy(
+                    wu_codes[b][:].rearrange("p a (t g m) -> p a g t m", t=PACK, m=4),
+                    wu_raw[b][:].rearrange("p a (g m t) -> p a g t m", t=PACK, m=4),
+                )
             else:
                 wu_codes[b] = staged("wu_codes1", [P, PASSES, PASS], I32, AT_WU1_CODES)
-                copy, walk = nc.gpsimd.tensor_copy, "p a t m"
-            copy(
-                wu_codes[b][:].rearrange("p a (t m) -> " + walk, t=PACK),
-                wu_raw[b][:].rearrange("p a (m t) -> " + walk, t=PACK),
-            )
+                nc.gpsimd.tensor_copy(
+                    wu_codes[b][:].rearrange("p a (t m) -> p a t m", t=PACK),
+                    wu_raw[b][:].rearrange("p a (m t) -> p a t m", t=PACK),
+                )
 
         wg_codes, wg_scale = {}, {}
 
@@ -314,8 +316,8 @@ def tile_list_modp_gsilu_gateP_kernel(
         hidden(2)
         wd_codes = staged("wd_codes", [P, PASSES, 2 * N], U8, AT_WD_CODES)
         nc.scalar.copy(
-            wd_codes[:].bitcast(U16).rearrange("p a (t m) -> p a m t", t=PACK),
-            wd_raw[:].bitcast(U16).rearrange("p a (m t) -> p a m t", t=PACK),
+            wd_codes[:].bitcast(U16).rearrange("p a (t g m) -> p a g t m", t=PACK, m=8),
+            wd_raw[:].bitcast(U16).rearrange("p a (g m t) -> p a g t m", t=PACK, m=8),
         )
         load_gate(3, AT_GATE3)
         gather_gate(2)
@@ -356,19 +358,19 @@ def tile_list_modp_gsilu_gateP_kernel(
                     copy = nc.vector.tensor_copy if piece < VECTOR_PIECES else nc.scalar.copy
                     copy(out_bf[:, c0:c1, PLANE[u]], page[u][:, c0:c1])
 
-        out_scale = sb("out_scale", [P, T], U8)
+        out_scale = sb("out_scale", [P, T // 2], U8)
         out_words = out_1[0].rearrange("p t i -> p (t i)").bitcast(I32)
         for piece, (c0, c1) in enumerate(pieces):
             codes = sb(f"out_codes{piece}", [P, c1 - c0], I32)
             nc.vector.quantize_mx(
                 out=codes[:].bitcast(FP8X4),
-                scales=out_scale[:, c0:c1],
+                scales=out_scale[4 * (c0 // (T // 2)) :, c0 % (T // 2) : c0 % (T // 2) + c1 - c0],
                 in_=out_bf[:, c0:c1, :].rearrange("p c t -> p (c t)"),
             )
             nc.sync.dma_start(out_words[:, c0:c1], codes[:])
         for quad in range(P // QUAD):
             queue = nc.scalar if quad // 2 else nc.sync
             queue.dma_start(
-                out_2[0, 4 * quad : 4 * quad + 4, :].bitcast(I32),
-                out_scale[QUAD * quad : QUAD * quad + 4, :].bitcast(I32),
+                out_2[0, 4 * quad : 4 * quad + 4, :].bitcast(I32).rearrange("r (k c) -> k r c", k=2),
+                out_scale[QUAD * quad : QUAD * quad + 8, :].bitcast(I32),
             )

@@ -43,8 +43,8 @@ AT_WU1_CODES = AT_GATE0 + 4
 AT_PAGE2, AT_ROUNDED10, AT_GATE2 = 110, 116, 118
 AT_PAGE = (AT_PAGE0, AT_PAGE1, AT_PAGE2)
 
-RUNS = ((0, 4, AT_GATE0), (4, 7, 73.75), (7, 9, 76.5), (9, 12, 78.25), (12, 16, 81))
-AT_GATED = (66, 70, 74, 82)
+RUNS = ((0, 4, 126), (4, 7, 73.75), (7, 9, 76.5), (9, 12, 78.25), (12, 16, 81))
+AT_GATED = (66, AT_WG01, 0, 20)
 AT_WEIGHED1 = 78
 GPSIMD_STEPS = {7: AT_WG11, 8: 0, 9: 4, 10: 8, 13: 12, 14: 16, 15: 20}
 ACT_ON_WG01 = 6
@@ -79,6 +79,10 @@ def tile_list_modp_gsilu_gateP_kernel(
 
         offsets = keep.tile([P, J // GROUP], U16, name="offsets")
         nc.sync.dma_start(offsets[:], offs)
+
+        warm = sb("warm", [P, 2], F32)
+        nc.vector.memset(warm[:, 0:1], 0.0)
+        nc.scalar.activation(warm[:, 1:2], warm[:, 0:1], SILU)
 
         ts_raw = sb("ts_raw", [P, T], U8)
         ws_raw = staged("ws_raw", [P, R], U8, AT_WEIGHT_SCALES)
@@ -135,6 +139,8 @@ def tile_list_modp_gsilu_gateP_kernel(
 
         load_wg(0, 0, AT_WG00)
         load_wg(1, 0, AT_WG10)
+        wd_raw = sb("wd_raw", [P, PASSES, 2 * N], U8)
+        nc.sync.dma_start(wd_raw[:].bitcast(I32), wd_words.rearrange("a p n -> p a n").bitcast(I32))
 
         ts_picked = staged("ts_picked", [P, J], U8, AT_PICKED_SCALES)
         nc.vector.tensor_copy(ts_picked[:], ts_raw[:].indirect(offsets[:]))
@@ -294,13 +300,16 @@ def tile_list_modp_gsilu_gateP_kernel(
             nc.vector.tensor_copy(page[u][:].indirect(offsets[:, j0 // GROUP : j1 // GROUP]), z[u][:, j0:j1])
 
         quantise_wg(0, 0)
-        load_wu(1)
         load_wg(0, 1, AT_WG01)
+        load_wu(1)
         load_wg(1, 1, AT_WG11)
         deal_wu(0)
         quantise_wg(1, 0)
-        wd_raw = staged("wd_raw", [P, PASSES, 2 * N], U8, AT_WD)
-        nc.sync.dma_start(wd_raw[:].bitcast(I32), wd_words.rearrange("a p n -> p a n").bitcast(I32))
+        wd_codes = sb("wd_codes", [P, PASSES, 2 * N], U8)
+        nc.scalar.copy(
+            wd_codes[:].bitcast(U16).rearrange("p a (t g m) -> p a g t m", t=PACK, m=8),
+            wd_raw[:].bitcast(U16).rearrange("p a (g m t) -> p a g t m", t=PACK, m=8),
+        )
         load_gate(1, AT_GATE1)
         load_gate(2, AT_GATE2)
         zero_page(2)
@@ -314,11 +323,6 @@ def tile_list_modp_gsilu_gateP_kernel(
         hidden(1)
         gather_gate(1)
         hidden(2)
-        wd_codes = staged("wd_codes", [P, PASSES, 2 * N], U8, AT_WD_CODES)
-        nc.scalar.copy(
-            wd_codes[:].bitcast(U16).rearrange("p a (t g m) -> p a g t m", t=PACK, m=8),
-            wd_raw[:].bitcast(U16).rearrange("p a (g m t) -> p a g t m", t=PACK, m=8),
-        )
         load_gate(3, AT_GATE3)
         gather_gate(2)
         hidden(3)

from contextlib import ExitStack

import concourse.mybir as mybir
from concourse.masks import make_identity

K, R, N, T, J = 1024, 1024, 512, 2048, 1024
FLOPS = 2 * J * (2 * K * R + R * N)

F32 = mybir.dt.float32
BF16 = mybir.dt.bfloat16
I32 = mybir.dt.int32
U32 = mybir.dt.uint32
U16 = mybir.dt.uint16
U8 = mybir.dt.uint8
FP8X4 = mybir.dt.float8_e4m3fn_x4
FP4X4 = mybir.dt.float4_e2m1fn_x4
MULT = mybir.AluOpType.mult
SILU = mybir.ActivationFunctionType.Silu

P = 128
PACK = 4
PASS = P * PACK
PASSES = 2
QUAD = 32
HALF = J // 2
GROUP = 16

PLANE = (2, 0, 1, 3)

EDGES = (0, 512, 1024, 1536, 1792, 2048)
VECTOR_PIECES = 2

AT_TAB_WORDS, AT_PICKED_WORDS = 0, 8
AT_WG10, AT_WD, AT_GATE1 = 24, 28, 30
AT_WG01, AT_WG00, AT_WU1 = 38, 44, 46
AT_WG11, AT_ROUNDED00 = 50, 52
AT_GATE3 = AT_WG11
AT_PAGE0 = 58
AT_ROUNDED11, AT_WD_CODES = 86, 86
AT_PAGE1, AT_PICKED_SCALES, AT_WU0 = 90, 97.5, 98
AT_WEIGHT_SCALES, AT_GATE0 = 101.5, 102
AT_WU1_CODES = AT_GATE0 + 4
AT_PAGE2, AT_ROUNDED10, AT_GATE2 = 110, 116, 118
AT_PAGE = (AT_PAGE0, AT_PAGE1, AT_PAGE2)

RUNS = ((0, 4, 126), (4, 7, 73.75), (7, 9, 76.5), (9, 12, 78.25), (12, 16, 81))
AT_GATED = (66, AT_WG01, 0, 20)
AT_WEIGHED1 = 78
GPSIMD_STEPS = {7: AT_WG11, 8: 0, 9: 4, 10: 8, 13: 12, 14: 16, 15: 20}
ACT_ON_WG01 = 6

GA_BANKS, UB_BANKS = 3, 5


def tile_list_modp_gsilu_gateP_kernel(
    tc, tab_words, tab_scales, wg, wu_words, wu_scales, wd_words, wd_scales, gT, wgo, offs, out_0, out_1, out_2
):
    nc = tc.nc
    with ExitStack() as ctx:
        keep = ctx.enter_context(tc.tile_pool(name="keep", bufs=1))
        shared = ctx.enter_context(tc.tile_pool(name="shared", bufs=1))
        ring = ctx.enter_context(tc.tile_pool(name="ring", bufs=3))
        psum = ctx.enter_context(tc.psum_pool(name="psum", bufs=1))

        def sb(name, shape, dtype, tag=None):
            return keep.tile(shape, dtype, name=name, tag=tag or name, align_bytes=64)

        def staged(name, shape, dtype, kib):
            return shared.tile(shape, dtype, name=name, offset=int(1024 * kib), align_bytes=64)

        def bank(name, number):
            return psum.tile([P, HALF], F32, name=name, offset=2048 * number)

        def ga_bank(step):
            return step % GA_BANKS

        def ub_bank(step):
            return GA_BANKS + step % UB_BANKS

        offsets = keep.tile([P, J // GROUP], U16, name="offsets")
        nc.sync.dma_start(offsets[:], offs)

        warm = sb("warm", [P, 2], F32)
        nc.vector.memset(warm[:, 0:1], 0.0)
        nc.scalar.activation(warm[:, 1:2], warm[:, 0:1], SILU)

        ts_raw = sb("ts_raw", [P, T], U8)
        ws_raw = staged("ws_raw", [P, R], U8, AT_WEIGHT_SCALES)
        nc.sync.dma_start(ts_raw[96:128, :].bitcast(I32), tab_scales.rearrange("a q t -> q a t").bitcast(I32))
        nc.sync.dma_start(ws_raw[96:128, :].bitcast(I32), wu_scales.rearrange("a q r -> q a r").bitcast(I32))
        nc.sync.dma_start(ws_raw[64:96, 0:N].bitcast(I32), wd_scales.rearrange("a q n -> q a n").bitcast(I32))
        nc.vector.memset(ts_raw[0:96, :].bitcast(I32), 0)
        nc.vector.memset(ws_raw[0:64, :].bitcast(I32), 0)
        nc.vector.memset(ws_raw[64:96, N:R].bitcast(I32), 0)

        wgo_row = sb("wgo_row", [P, J // P], F32)
        nc.sync.dma_start(wgo_row[:], wgo[0].rearrange("(p c) -> p c", p=P))
        identity = sb("identity", [P, P], F32)
        make_identity(nc, identity[:])
        wgo_sb = sb("wgo_sb", [P, J], F32)
        for g in range(J // HALF):
            spread = bank(f"spread{g}", ub_bank(3 + g))
            for c in range(PACK):
                column = wgo_row[:, PACK * g + c : PACK * g + c + 1]
                nc.tensor.transpose(spread[:, P * c : P * (c + 1)], column.to_broadcast([P, P]), identity[:])
            nc.scalar.copy(
                wgo_sb[:].rearrange("p (k g c) -> p g k c", g=J // HALF, c=PACK)[:, g],
                spread[:].rearrange("p (c k) -> p k c", c=PACK),
            )

        def place_scale_rows(scale, rows):
            for quad in (0, 2, 1, 3):
                nc.sync.dma_start(
                    scale[QUAD * quad : QUAD * quad + 4].bitcast(I32), rows[8 * quad : 8 * (quad + 1)].bitcast(I32)
                )

        tab_raw = staged("tab_raw", [P, T], I32, AT_TAB_WORDS)
        nc.sync.dma_start(tab_raw[:], tab_words[0].rearrange("p t i -> p (t i)").bitcast(I32))

        wg_raw = {}

        def load_wg(a, b, kib):
            wg_raw[a, b] = staged(f"wg_raw{a}{b}", [P, PACK, PASS], F32, kib)
            rows = wg[PASS * a : PASS * (a + 1), PASS * b : PASS * (b + 1)]
            nc.sync.dma_start(wg_raw[a, b][:], rows.rearrange("(p i) c -> p i c", i=PACK))

        wu_raw = {}

        def load_wu(b):
            wu_raw[b] = staged(f"wu_raw{b}", [P, PASSES, PASS], I32, (AT_WU0, AT_WU1)[b])
            words = wu_words.rearrange("a p r i -> p a (r i)")
            nc.sync.dma_start(wu_raw[b][:], words[:, :, PACK * PASS * b : PACK * PASS * (b + 1)].bitcast(I32))

        gate_raw = {}

        def load_gate(u, kib):
            gate_raw[u] = staged(f"gate_raw{u}", [P, T], F32, kib)
            nc.sync.dma_start(gate_raw[u][:], gT.rearrange("(p t) c -> p t c", t=PACK)[:, PLANE[u], :])

        load_wg(0, 0, AT_WG00)
        load_wg(1, 0, AT_WG10)
        wd_raw = sb("wd_raw", [P, PASSES, 2 * N], U8)
        nc.sync.dma_start(wd_raw[:].bitcast(I32), wd_words.rearrange("a p n -> p a n").bitcast(I32))

        ts_picked = staged("ts_picked", [P, J], U8, AT_PICKED_SCALES)
        nc.vector.tensor_copy(ts_picked[:], ts_raw[:].indirect(offsets[:]))
        page = {}

        def zero_page(u):
            page[u] = staged(f"page{u}", [P, T], F32, AT_PAGE[u])
            nc.gpsimd.memset(page[u][:].bitcast(I32), 0)

        zero_page(0)

        scale_rows = sb("scale_rows", [P, R + J], U8)
        nc.gpsimd.tensor_copy(
            scale_rows[:, 0:R].rearrange("p (b t m) -> p b t m", b=R // PASS, t=PACK),
            ws_raw[:].rearrange("p (b m t) -> p b t m", b=R // PASS, t=PACK),
        )
        nc.vector.tensor_copy(scale_rows[96:128, R:].bitcast(I32), ts_picked[96:128, :].bitcast(I32))
        placed = sb("placed", [P, PASSES, R + J], U8)
        place_scale_rows(placed, scale_rows[96:128, :])
        wu_scale, tab_scale = placed[:, :, 0:R], placed[:, :, R:]
        load_wu(0)
        zero_page(1)

        tab_picked = staged("tab_picked", [P, J], I32, AT_PICKED_WORDS)
        for j0 in range(0, J, HALF):
            listed = tab_raw[:].bitcast(U32).indirect(offsets[:, j0 // GROUP : (j0 + HALF) // GROUP])
            nc.vector.tensor_copy(tab_picked[:, j0 : j0 + HALF].bitcast(U32), listed)
        load_gate(0, AT_GATE0)
        tab_codes = [sb(f"tab_codes{half}", [P, PASSES, 2 * HALF], U8) for half in range(J // HALF)]
        for half in range(J // HALF):
            words = tab_picked[:, HALF * half : HALF * (half + 1)].bitcast(U16)
            nc.vector.tensor_copy(tab_codes[half][:].bitcast(U16), words.rearrange("p (j a) -> p a j", a=PASSES))

        wu_codes = {}

        def deal_wu(b):
            if b == 0:
                wu_codes[b] = sb("wu_codes0", [P, PASSES, PASS], I32)
                nc.vector.tensor_copy(
                    wu_codes[b][:].rearrange("p a (t g m) -> p a g t m", t=PACK, m=4),
                    wu_raw[b][:].rearrange("p a (g m t) -> p a g t m", t=PACK, m=4),
                )
            else:
                wu_codes[b] = staged("wu_codes1", [P, PASSES, PASS], I32, AT_WU1_CODES)
                nc.gpsimd.tensor_copy(
                    wu_codes[b][:].rearrange("p a (t m) -> p a t m", t=PACK),
                    wu_raw[b][:].rearrange("p a (m t) -> p a t m", t=PACK),
                )

        wg_codes, wg_scale = {}, {}

        def quantise_wg(a, b):
            if (a, b) == (0, 1):
                rounded = sb("wg_bf01", [P, PACK * PASS], BF16)
            else:
                kib = {(0, 0): AT_ROUNDED00, (1, 0): AT_ROUNDED10, (1, 1): AT_ROUNDED11}[a, b]
                rounded = staged(f"wg_bf{a}{b}", [P, PACK * PASS], BF16, kib)
            dst = rounded[:].rearrange("p (t m i) -> p m i t", t=PACK, i=PACK)
            src = wg_raw[a, b][:].rearrange("p i (m t) -> p m i t", t=PACK)
            nc.scalar.copy(dst[:, 0 : P // 2], src[:, 0 : P // 2])
            copy = nc.vector.tensor_copy if a == 1 else nc.scalar.copy
            copy(dst[:, P // 2 : P], src[:, P // 2 : P])
            if (a, b) == (1, 0):
                wg_codes[a, b] = staged("wg_codes10", [P, PASS], U32, AT_WU0)
            else:
                wg_codes[a, b] = sb(f"wg_codes{a}{b}", [P, PASS], U32)
            wg_scale[a, b] = sb(f"wg_scale{a}{b}", [P, PASS], U8)
            nc.vector.quantize_mx(out=wg_codes[a, b][:].bitcast(FP8X4), scales=wg_scale[a, b][:], in_=rounded[:])

        gate = {}

        def gather_gate(u):
            gate[u] = staged(f"gate{u}", [P, J], F32, AT_GATED[u])
            if u == 0:
                nc.vector.tensor_tensor(gate[u][:], gate_raw[u][:].indirect(offsets[:]), wgo_sb[:], MULT)
            else:
                nc.vector.tensor_copy(gate[u][:], gate_raw[u][:].indirect(offsets[:]))

        h_codes = sb("h_codes", [P, PASSES * J], U32)
        h_scale = sb("h_scale", [P, PASSES * J], U8)

        def hidden(run, ahead_of_last=None):
            first, end, kib = RUNS[run]
            rounded = staged(f"h_bf{run}", [P, PACK * P * (end - first)], BF16, kib)
            for step in range(first, end):
                b, j0 = divmod(P * step, J)
                half, s = j0 // HALF, j0 % HALF // P
                out = rounded[:, PACK * P * (step - first) : PACK * P * (step - first + 1)]
                if step == end - 1 and ahead_of_last:
                    ahead_of_last()
                ga = bank(f"ga{step}", ga_bank(step))
                ub = bank(f"ub{step}", ub_bank(step))
                for a in range(PASSES):
                    for t in range(PACK):
                        nc.tensor.matmul_mx(
                            out=ga[:, P * t : P * (t + 1)],
                            lhsT=wg_codes[a, b][:, P * t : P * (t + 1)].bitcast(FP8X4),
                            lhsT_scale=wg_scale[a, b][:, P * t : P * (t + 1)],
                            rhs=tab_codes[half][:, a, 2 * P * s : 2 * P * (s + 1)].bitcast(FP4X4),
                            rhs_scale=tab_scale[:, a, j0 : j0 + P],
                            start=(a, t) == (0, 0),
                            stop=(a, t) == (PASSES - 1, PACK - 1),
                        )
                for t in range(PACK):
                    for a in range(PASSES):
                        nc.tensor.matmul_mx(
                            out=ub[:, P * t : P * (t + 1)],
                            lhsT=wu_codes[b][:, a, P * t : P * (t + 1)].bitcast(FP8X4),
                            lhsT_scale=wu_scale[:, a, PASS * b + P * t : PASS * b + P * (t + 1)],
                            rhs=tab_codes[half][:, a, 2 * P * s : 2 * P * (s + 1)].bitcast(FP4X4),
                            rhs_scale=tab_scale[:, a, j0 : j0 + P],
                            start=(a == 0),
                            stop=(a == PASSES - 1),
                        )
                ga_walk = ga[:].rearrange("p (t c e) -> p c t e", t=PACK, e=2)
                ub_walk = ub[:].rearrange("p (t c e) -> p c t e", t=PACK, e=2)
                interleaved = "p (c e t) -> p c t e"
                if step in GPSIMD_STEPS:
                    act = staged(f"act{step}", [P, PACK * P], F32, GPSIMD_STEPS[step])
                    ub_sb = staged(f"ub_sb{step}", [P, PACK * P], F32, GPSIMD_STEPS[step] + 2)
                    nc.scalar.activation(act[:].rearrange(interleaved, t=PACK, e=2), ga_walk, SILU)
                    nc.scalar.copy(ub_sb[:].rearrange(interleaved, t=PACK, e=2), ub_walk)
                    nc.gpsimd.tensor_tensor(out, ub_sb[:], act[:], MULT)
                else:
                    if step == ACT_ON_WG01:
                        act = staged(f"act{step}", [P, P // 2, PACK, 2], F32, AT_WG01)
                    else:
                        act = ring.tile([P, P // 2, PACK, 2], F32, name="act")
                    nc.scalar.activation(act[:], ga_walk, SILU)
                    nc.vector.tensor_tensor(out.rearrange(interleaved, t=PACK, e=2), ub_walk, act[:], MULT)
            words = slice(P * first, P * end)
            nc.vector.quantize_mx(out=h_codes[:, words].bitcast(FP8X4), scales=h_scale[:, words], in_=rounded[:])

        y_sb = {u: sb(f"y_sb{u}", [P, J], F32) for u in range(1, PACK)}
        z = {u: sb(f"z{u}", [P, J], F32) for u in range(PACK)}

        def down(u, half, number):
            y = bank(f"y{u}{half}", number)
            n0 = P * PLANE[u]
            for a in range(PASSES):
                nc.tensor.matmul_mx(
                    out=y[:],
                    lhsT=wd_codes[:, a, 2 * n0 : 2 * (n0 + P)].bitcast(FP4X4),
                    lhsT_scale=wd_scale[:, a, n0 : n0 + P],
                    rhs=h_codes[:, J * a + HALF * half : J * a + HALF * (half + 1)].bitcast(FP8X4),
                    rhs_scale=h_scale[:, J * a + HALF * half : J * a + HALF * (half + 1)],
                    start=(a == 0),
                    stop=(a == PASSES - 1),
                )
            cols = slice(HALF * half, HALF * (half + 1))
            if u == 0:
                nc.vector.tensor_tensor(z[0][:, cols], y[:], gate[0][:, cols], MULT)
            else:
                nc.scalar.copy(y_sb[u][:, cols], y[:])

        def scatter(u, j0, j1):
            nc.vector.tensor_copy(page[u][:].indirect(offsets[:, j0 // GROUP : j1 // GROUP]), z[u][:, j0:j1])

        quantise_wg(0, 0)
        load_wg(0, 1, AT_WG01)
        load_wu(1)
        load_wg(1, 1, AT_WG11)
        deal_wu(0)
        quantise_wg(1, 0)
        wd_codes = sb("wd_codes", [P, PASSES, 2 * N], U8)
        nc.scalar.copy(
            wd_codes[:].bitcast(U16).rearrange("p a (t g m) -> p a g t m", t=PACK, m=8),
            wd_raw[:].bitcast(U16).rearrange("p a (g m t) -> p a g t m", t=PACK, m=8),
        )
        load_gate(1, AT_GATE1)
        load_gate(2, AT_GATE2)
        zero_page(2)
        gather_gate(0)
        deal_wu(1)
        hidden(0)
        quantise_wg(0, 1)
        quantise_wg(1, 1)
        wd_scale = sb("wd_scale", [P, PASSES, N], U8, tag="wg_bf01")
        place_scale_rows(wd_scale, scale_rows[64:96, 0:N])
        hidden(1)
        gather_gate(1)
        hidden(2)
        load_gate(3, AT_GATE3)
        gather_gate(2)
        hidden(3)

        def first_scatter():
            down(0, 0, ub_bank(13))
            scatter(0, 0, HALF)

        hidden(4, first_scatter)
        for u, step in zip(range(1, PACK), (11, 12, 14)):
            down(u, 0, ub_bank(step))
        gather_gate(3)
        for u, number in enumerate((ga_bank(13), ga_bank(14), ga_bank(15), ub_bank(15))):
            down(u, 1, number)

        pieces = list(zip(EDGES[:-1], EDGES[1:]))
        out_bf = sb("out_bf", [P, T, PACK], BF16, tag="h_codes")
        out_rows = out_0.rearrange("(p t) c -> p t c", t=PACK)
        last = PACK - 1
        for u in range(PACK):
            if u == last:
                page[u] = page[0]
            if u > 0:
                if u == 1:
                    weighed = staged("weighed1", [P, J], F32, AT_WEIGHED1)
                else:
                    weighed = sb(f"weighed{u}", [P, J], F32, tag=f"y_sb{u - 1}")
                nc.gpsimd.tensor_tensor(weighed[:], gate[u][:], wgo_sb[:], MULT)
                nc.gpsimd.tensor_tensor(z[u][:], y_sb[u][:], weighed[:], MULT)
            scatter(u, HALF if u == 0 else 0, J)
            queue = nc.scalar if u == last else nc.sync
            queue.dma_start(out_rows[:, PLANE[u], :], page[u][:])
            if u < last:
                nc.scalar.copy(out_bf[:, :, PLANE[u]], page[u][:])
            else:
                for piece, (c0, c1) in enumerate(pieces):
                    copy = nc.vector.tensor_copy if piece < VECTOR_PIECES else nc.scalar.copy
                    copy(out_bf[:, c0:c1, PLANE[u]], page[u][:, c0:c1])

        out_scale = sb("out_scale", [P, T // 2], U8)
        out_words = out_1[0].rearrange("p t i -> p (t i)").bitcast(I32)
        for piece, (c0, c1) in enumerate(pieces):
            codes = sb(f"out_codes{piece}", [P, c1 - c0], I32)
            nc.vector.quantize_mx(
                out=codes[:].bitcast(FP8X4),
                scales=out_scale[4 * (c0 // (T // 2)) :, c0 % (T // 2) : c0 % (T // 2) + c1 - c0],
                in_=out_bf[:, c0:c1, :].rearrange("p c t -> p (c t)"),
            )
            nc.sync.dma_start(out_words[:, c0:c1], codes[:])
        for quad in range(P // QUAD):
            queue = nc.scalar if quad // 2 else nc.sync
            queue.dma_start(
                out_2[0, 4 * quad : 4 * quad + 4, :].bitcast(I32).rearrange("r (k c) -> k r c", k=2),
                out_scale[QUAD * quad : QUAD * quad + 8, :].bitcast(I32),
            )
